import numpy as np
import ml_dtypes


def mxq(x, axis, fmt="e4m3"):
    dtype, down = {"e4m3": (ml_dtypes.float8_e4m3fn, 7), "e5m2": (ml_dtypes.float8_e5m2, 14)}[fmt]
    v = np.moveaxis(np.asarray(x, np.float32).astype(ml_dtypes.bfloat16).astype(np.float64), axis, -1)
    blocks = v.reshape(v.shape[:-1] + (-1, 32))
    amax = np.abs(blocks).max(-1, keepdims=True)
    byte = np.maximum(np.where(amax > 0, np.frexp(amax)[1] - 1 + 127, 0) - down, 1)
    scale = np.exp2(byte - 127.0)
    codes = (blocks / scale).astype(np.float32).astype(dtype).astype(np.float64)
    return np.moveaxis((codes * scale).reshape(v.shape), -1, axis)


WIDE = False


def mx_kscale(k):
    if not WIDE:
        return np.ones(k)
    levels = np.array([10, -10, 5, -5, 0])
    if k % 512:
        return np.exp2(np.random.permutation(np.resize(levels, k // 32))).repeat(32)
    a = np.empty((k // 512, 16))
    for p in range(k // 512):
        a[p, :8] = np.random.permutation(np.resize(levels, 8))
        for g in range(8):
            far = levels[np.abs(levels - a[p, g]) >= 10]
            a[p, g + 8] = far[np.random.randint(len(far))]
    return np.exp2(a.ravel()).repeat(32)


def f64(x):
    return np.asarray(x).astype(np.float64)


def striped(idx):
    return np.tile(idx.reshape(-1, 16).T, (8, 1)).astype(np.uint16)


def unstriped(offs):
    return offs[:16].T.reshape(-1).astype(np.int64)


E2M1 = np.array([0.0, 0.5, 1.0, 1.5, 2.0, 3.0, 4.0, 6.0, -0.0, -0.5, -1.0, -1.5, -2.0, -3.0, -4.0, -6.0])


def pack_weight(w, fmt):
    k, n = w.shape
    w = f64(np.asarray(w, np.float32).astype(ml_dtypes.bfloat16)).reshape(k // 32, 32, n)
    amax = np.abs(w).max(1)
    if fmt == "e4m3":
        byte = np.frexp(amax)[1] - 1 + 127 - 7
    else:
        mant, ex = np.frexp(amax / 6.0)
        byte = np.where(mant > 0.5, ex, ex - 1) + 127
    byte = np.clip(np.where(amax > 0, byte, 1), 1, 254)
    scaled = (w * np.exp2(127.0 - byte)[:, None, :]).reshape(k, n).astype(np.float32)
    by_word = np.ascontiguousarray(scaled.reshape(k // 512, 128, 4, n).transpose(0, 1, 3, 2))
    if fmt == "e4m3":
        words = by_word.astype(ml_dtypes.float8_e4m3fn).view(np.uint8)
    else:
        c = by_word.astype(ml_dtypes.float4_e2m1fn).view(np.uint8) & 0xF
        words = (c[..., 0::2] | (c[..., 1::2] << 4)).reshape(k // 512, 128, 2 * n)
    return np.ascontiguousarray(words), np.ascontiguousarray(byte.astype(np.uint8).reshape(k // 512, 16, n))


def unpack_weight(words, scales, fmt):
    g, _, n = scales.shape
    words = np.ascontiguousarray(words).reshape(g, 128, n, -1)
    if fmt == "e4m3":
        vals = words.view(ml_dtypes.float8_e4m3fn).astype(np.float64)
    else:
        nib = np.empty((g, 128, n, 4), np.uint8)
        nib[..., 0::2] = words & 0xF
        nib[..., 1::2] = words >> 4
        vals = E2M1[nib]
    vals = vals * np.repeat(np.exp2(scales.astype(np.float64) - 127.0), 8, axis=1)[..., None]
    return vals.transpose(0, 1, 3, 2).reshape(g * 512, n)


def gelu(v):
    return 0.5 * v * (1.0 + np.tanh(np.sqrt(2.0 / np.pi) * (v + 0.044715 * v**3)))


def bf(x):
    return np.asarray(x, np.float32).astype(ml_dtypes.bfloat16)


def planes(Y):
    n, m = Y.shape
    b = f64(bf(Y)).reshape(n // 32, 32, m)
    amax = np.abs(b).max(1)
    byte = np.clip(np.where(amax > 0, np.frexp(amax)[1] - 1 + 127 - 7, 1), 1, 254)
    codes = (b * np.exp2(127.0 - byte)[:, None, :]).reshape(n, m).astype(np.float32).astype(ml_dtypes.float8_e4m3fn).view(np.uint8)
    words = codes.reshape(n // 512, 128, 4, m).transpose(0, 1, 3, 2)
    return np.ascontiguousarray(words), np.ascontiguousarray(byte.astype(np.uint8).reshape(n // 512, 16, m))


K, T, H, S, T2, P = 1536, 2048, 1024, 512, 1024, 512

def setup_inputs():
    n = np.random.standard_normal
    s = mx_kscale(K)[:, None]
    u = mx_kscale(H)[:, None]
    d = {}
    d["tab_words"], d["tab_scales"] = pack_weight(n((K, T)) * s, "e4m3")
    d["w1_words"], d["w1_scales"] = pack_weight(n((K, H)) / s / K ** 0.5, "e4m3")
    d["gain"] = (np.exp(0.3 * n(H)) * u[:, 0]).astype(np.float32)
    d["page0"] = (n((H, T2)) * u).astype(np.float32)
    d["wgs"] = np.exp(0.3 * n((128, S))).astype(np.float32)
    d["rs"] = (np.exp(0.5 * n(H)) / u[:, 0]).astype(np.float32)
    d["gx"] = (np.exp(0.3 * n(H)) * u[:, 0]).astype(np.float32)
    d["w2_words"], d["w2_scales"] = pack_weight(n((H, H)) / u * np.exp(0.8 * n(H)) / H ** 0.5, "e2m1")
    d["w3"] = (0.75 * n((H, H)) / u / H ** 0.5).astype(np.float32)
    d["offs"] = striped(np.random.permutation(T)[:S])
    d["offs2"] = striped(np.random.permutation(T2)[:S])
    d["offs3"] = striped(np.random.permutation(T2)[:P])
    d["offs4"] = striped(np.random.permutation(T2)[:P])
    return d

def reference(tab_words, tab_scales, w1_words, w1_scales, gain, page0, wgs, rs, gx,
              w2_words, w2_scales, w3, offs, offs2, offs3, offs4):
    v = unpack_weight(tab_words, tab_scales, "e4m3")[:, unstriped(offs)]
    w1 = unpack_weight(w1_words, w1_scales, "e4m3")
    h = f64(gain)[:, None] * (w1.T @ v)
    page = f64(page0).copy()
    page[:, unstriped(offs2)] = np.tile(f64(wgs), (H // 128, 1)) * h
    board = f64(rs)[:, None] * page
    x = f64(gx)[:, None] * np.tanh(board[:, unstriped(offs3)])
    xq = mxq(x, 0, "e4m3")
    w2 = unpack_weight(w2_words, w2_scales, "e2m1")
    growth = w2.T @ xq
    season = mxq(f64(w3), 0, "e4m3").T @ xq
    y = growth * np.cos(season) + board[:, unstriped(offs4)]
    words, scales = planes(y)
    return y, words, scales

@@ -1,0 +1,297 @@
+import math
+from contextlib import ExitStack
+
+import concourse.mybir as mybir
+from concourse.masks import make_identity
+
+K, T, H, S, T2, PICKS = 1536, 2048, 1024, 512, 1024, 512
+FLOPS = 2 * K * H * S + 2 * 2 * H * H * PICKS
+
+F32 = mybir.dt.float32
+BF16 = mybir.dt.bfloat16
+I32 = mybir.dt.int32
+U32 = mybir.dt.uint32
+U16 = mybir.dt.uint16
+U8 = mybir.dt.uint8
+FP8X4 = mybir.dt.float8_e4m3fn_x4
+FP4X4 = mybir.dt.float4_e2m1fn_x4
+ACT = mybir.ActivationFunctionType
+ALU = mybir.AluOpType
+
+P = 128
+PACK = 4
+PASS = P * PACK
+QUADS = 4
+K_PASSES = K // PASS
+GROUPS = H // PASS
+SLICES = GROUPS * PACK
+BLOCKS = PICKS // P
+
+
+def tile_list_kelp_harvest_planner_kernel(
+    tc, tab_words, tab_scales, w1_words, w1_scales, gain, page0, wgs, rs, gx,
+    w2_words, w2_scales, w3, offs, offs2, offs3, offs4, out_0, out_1, out_2,
+):
+    nc = tc.nc
+    with ExitStack() as ctx:
+        lists = ctx.enter_context(tc.tile_pool(name="lists", bufs=1))
+        keep = ctx.enter_context(tc.tile_pool(name="keep", bufs=1))
+        ring = ctx.enter_context(tc.tile_pool(name="ring", bufs=2))
+        psum = ctx.enter_context(tc.psum_pool(name="psum", bufs=1))
+
+        def load_list(source, name):
+            tile = lists.tile([P, S // 16], U16, name=name)
+            nc.sync.dma_start(tile[:], source)
+            return tile
+
+        def load_rowvec(source, name):
+            tile = keep.tile([P, GROUPS, PACK], F32, name=name)
+            nc.gpsimd.dma_start(tile[:], source.rearrange("(g p t) -> p g t", g=GROUPS, t=PACK))
+            return tile
+
+        w1_cols = w1_words.rearrange("a p c i -> p a (c i)").bitcast(I32)
+        page_rows = page0.rearrange("(g p t) c -> g t p c", g=GROUPS, t=PACK)
+        wgs_rows = wgs.rearrange("(m t) s -> m t s", t=PACK)
+        w3_rows = w3.rearrange("(a p j) n -> a p j n", a=GROUPS, j=PACK)
+        out_rows = out_0.rearrange("(g p t) j -> g p t j", g=GROUPS, t=PACK)
+        out_words = out_1.rearrange("g p m t -> g p (m t)").bitcast(I32)
+
+        def load_w1(g):
+            tile = ring.tile([P, K_PASSES, PASS], I32, name="w1_raw", tag="w1_raw")
+            nc.sync.dma_start(tile[:], w1_cols[:, :, g * PASS:(g + 1) * PASS])
+            return tile
+
+        def load_page(s):
+            tile = keep.tile([P, T2], F32, name="page%d" % s)
+            nc.sync.dma_start(tile[:], page_rows[s // PACK, s % PACK])
+            return tile
+
+        def load_w3(q):
+            tile = ring.tile([P, PACK, PASS], F32, name="w3_raw", tag="big", bufs=4)
+            nc.sync.dma_start(tile[:], w3_rows[q // 2][:, :, (q % 2) * PASS:(q % 2 + 1) * PASS])
+            return tile
+
+        tab_plane = keep.tile([P, T], U8, tag="v_codes2", align_bytes=64)
+        w1_plane_raw = keep.tile([P, H], U8, tag="v_codes1", align_bytes=64)
+        w2_plane = keep.tile([P, GROUPS, H], U8, align_bytes=64)
+        warm = keep.tile([P, 8], F32)
+        nc.gpsimd.memset(tab_plane[:].bitcast(I32), 0)
+        nc.gpsimd.memset(w1_plane_raw[:].bitcast(I32), 0)
+        nc.vector.memset(warm[:], 0.0)
+        nc.vector.memset(w2_plane[:].bitcast(I32), 0)
+        for q in range(QUADS):
+            nc.scalar.dma_start(tab_plane[32 * q:32 * q + 4 * K_PASSES, :].bitcast(I32),
+                                tab_scales[:, 4 * q:4 * q + 4, :].bitcast(I32))
+        for q in range(QUADS):
+            nc.gpsimd.dma_start(w1_plane_raw[32 * q:32 * q + 4 * K_PASSES, :].bitcast(I32),
+                                w1_scales[:, 4 * q:4 * q + 4, :].bitcast(I32))
+        warm_out = keep.tile([P, 8], F32)
+        nc.scalar.activation(warm_out[:], warm[:], ACT.Silu)
+        gain_t = load_rowvec(gain, "gain_t")
+        rs_t = load_rowvec(rs, "rs_t")
+        gx_t = load_rowvec(gx, "gx_t")
+        for q in range(QUADS):
+            nc.gpsimd.dma_start(w2_plane[32 * q:32 * q + 4, :, :].bitcast(I32),
+                                w2_scales[:, 4 * q:4 * q + 4, :].rearrange("a r n -> r a n").bitcast(I32))
+        ident = keep.tile([P, P], F32)
+        make_identity(nc, ident[:])
+
+        idx = load_list(offs, "idx")
+        idx2 = load_list(offs2, "idx2")
+        idx3 = load_list(offs3, "idx3")
+        idx4 = load_list(offs4, "idx4")
+        w1_raw = [load_w1(0)]
+        tab = []
+        for a in range(K_PASSES):
+            tile = ring.tile([P, T], I32, name="tab", tag="big", bufs=4)
+            nc.sync.dma_start(tile[:], tab_words[a].rearrange("p c i -> p (c i)").bitcast(I32))
+            tab.append(tile)
+        pages = [load_page(0)]
+        wg_first = keep.tile([P, S], F32)
+        for q in range(QUADS):
+            nc.sync.dma_start(wg_first[32 * q:32 * q + 32, :], wgs_rows[:, 0, :])
+        wg_rest = keep.tile([P, PACK - 1, S], F32)
+        for q in range(QUADS):
+            nc.sync.dma_start(wg_rest[32 * q:32 * q + 32, :, :], wgs_rows[:, 1:PACK, :])
+        pages.append(load_page(1))
+        pages.append(load_page(2))
+        w1_raw.append(load_w1(1))
+        pages.append(load_page(3))
+        w3_raw = [load_w3(0)]
+        pages.append(load_page(4))
+        w3_raw.append(load_w3(1))
+        pages.append(load_page(5))
+        w3_raw.append(load_w3(2))
+        pages.append(load_page(6))
+        w3_raw.append(load_w3(3))
+        pages.append(load_page(7))
+        w2_codes = keep.tile([P, GROUPS, 2 * H], U8, align_bytes=64)
+        nc.sync.dma_start(w2_codes[:].bitcast(I32), w2_words.rearrange("a p b -> p a b").bitcast(I32))
+
+        def wg(t):
+            return wg_first[:] if t == 0 else wg_rest[:, t - 1, :]
+
+        w1_dealt = {}
+
+        def deal_w1(g):
+            for a in range(K_PASSES):
+                tile = keep.tile([P, PACK, P], I32, name="w1_dealt%d_%d" % (g, a), align_bytes=64)
+                nc.vector.tensor_copy(tile[:].rearrange("p t m -> p m t"),
+                                      w1_raw[g][:, a, :].rearrange("p (m t) -> p m t", t=PACK))
+                w1_dealt[g, a] = tile
+
+        deal_w1(0)
+        w1_plane = keep.tile([P, GROUPS, PACK, P], U8, align_bytes=64)
+        nc.vector.tensor_copy(w1_plane[:], w1_plane_raw[:].rearrange("p (g m t) -> p g t m", g=GROUPS, t=PACK))
+        v_plane = keep.tile([P, S], U8, align_bytes=64)
+        nc.vector.tensor_copy(v_plane[:], tab_plane[:].indirect(idx[:]))
+        v_codes = []
+        for a in range(K_PASSES):
+            tile = keep.tile([P, S], I32, name="v_codes%d" % a, tag="v_codes%d" % a, align_bytes=64)
+            nc.vector.tensor_copy(tile[:].bitcast(U32), tab[a][:].bitcast(U32).indirect(idx[:]))
+            v_codes.append(tile)
+
+        def put(s):
+            g, t = divmod(s, PACK)
+            bank = psum.tile([P, S], F32, name="h_bank", tag="early", bufs=2)
+            for a in range(K_PASSES):
+                nc.tensor.matmul_mx(
+                    out=bank[:], lhsT=w1_dealt[g, a][:, t, :].bitcast(FP8X4), lhsT_scale=w1_plane[4 * a:P, g, t, :],
+                    rhs=v_codes[a][:].bitcast(FP8X4), rhs_scale=v_plane[4 * a:P, :],
+                    start=(a == 0), stop=(a == K_PASSES - 1))
+            if s == SLICES - 1:
+                h = keep.tile([P, S], F32, name="h", tag="upstream4", align_bytes=64)
+            else:
+                h = ring.tile([P, S], F32, name="h", tag="h", bufs=3)
+            nc.scalar.activation(h[:], bank[:], ACT.Copy, scale=gain_t[:, g, t:t + 1])
+            nc.vector.tensor_tensor(pages[s][:].indirect(idx2[:]), h[:], wg(t), ALU.mult)
+
+        x_codes = [keep.tile([P, PICKS], I32, name="x_codes%d" % g, align_bytes=64) for g in range(GROUPS)]
+        x_plane = [keep.tile([P, PICKS], U8, name="x_plane%d" % g, align_bytes=64) for g in range(GROUPS)]
+        x_woven = [keep.tile([P, PICKS, PACK], BF16, name="x_woven%d" % g, tag="x_woven%d" % g, align_bytes=64)
+                   for g in range(GROUPS)]
+
+        def reread(s):
+            g, t = divmod(s, PACK)
+            picked = ring.tile([P, PICKS], F32, name="picked", tag="picked")
+            nc.vector.tensor_copy(picked[:], pages[s][:].indirect(idx3[:]))
+            bent = ring.tile([P, PICKS], F32, name="bent", tag="bent")
+            nc.scalar.activation(bent[:], picked[:], ACT.Tanh, scale=rs_t[:, g, t:t + 1])
+            pieces = BLOCKS if s == SLICES - 1 else 1
+            width = PICKS // pieces
+            for n in range(pieces):
+                cols = slice(n * width, (n + 1) * width)
+                nc.scalar.activation(x_woven[g][:, cols, t], bent[:, cols], ACT.Copy, scale=gx_t[:, g, t:t + 1])
+                if t == PACK - 1:
+                    nc.vector.quantize_mx(out=x_codes[g][:, cols].bitcast(FP8X4), scales=x_plane[g][:, cols],
+                                          in_=x_woven[g][:, cols, :].rearrange("p c t -> p (c t)"))
+
+        w3_codes = {}
+        w3_plane = {}
+
+        def quantise_w3(q):
+            woven = ring.tile([P, PASS, PACK], BF16, name="w3_woven", tag="woven", bufs=4, align_bytes=64)
+            for half in range(2):
+                cols = slice(half * PASS // 2, (half + 1) * PASS // 2)
+                nc.scalar.copy(woven[:, cols, :].rearrange("p (c i) t -> p c t i", i=4),
+                               w3_raw[q][:, :, cols].rearrange("p t (c i) -> p c t i", i=4))
+            key = divmod(q, 2)
+            w3_codes[key] = keep.tile([P, PASS], I32, name="w3_codes%d" % q, align_bytes=64)
+            w3_plane[key] = keep.tile([P, PASS], U8, name="w3_plane%d" % q, align_bytes=64)
+            nc.vector.quantize_mx(out=w3_codes[key][:].bitcast(FP8X4), scales=w3_plane[key][:],
+                                  in_=woven[:].rearrange("p c t -> p (c t)"))
+
+        upstream = {}
+
+        def fetch_upstream(s, tag):
+            upstream[s] = keep.tile([P, PICKS], F32, name="upstream%d" % s, tag=tag, align_bytes=64)
+            nc.vector.tensor_copy(upstream[s][:], pages[s][:].indirect(idx4[:]))
+
+        for s in range(SLICES):
+            if s == PACK - 1:
+                deal_w1(1)
+            put(s)
+            if s > 0:
+                reread(s - 1)
+            if 0 < s <= PACK:
+                fetch_upstream(s - 1, "upstream%d" % (s - 1))
+            if s >= PACK:
+                quantise_w3(s - PACK)
+        reread(SLICES - 1)
+        fetch_upstream(4, "upstream4")
+        fetch_upstream(5, "x_woven1")
+
+        y_codes = [keep.tile([P, PICKS], I32, name="y_codes%d" % g, align_bytes=64) for g in range(GROUPS)]
+        y_plane = keep.tile([P, GROUPS, PICKS], U8, align_bytes=64)
+        cosine = {}
+        growth = {}
+        turned = {}
+
+        def dealt(bank):
+            return bank[:].rearrange("j (m t) -> j t m", t=PACK)
+
+        def multiply(u):
+            g, b = divmod(u, BLOCKS)
+            cols = slice(b * P, (b + 1) * P)
+            season = psum.tile([P, PASS], F32, name="season", tag="early", bufs=2)
+            for a in range(GROUPS):
+                nc.tensor.matmul_mx(
+                    out=season[:], lhsT=x_codes[a][:, cols].bitcast(FP8X4), lhsT_scale=x_plane[a][:, cols],
+                    rhs=w3_codes[a, g][:].bitcast(FP8X4), rhs_scale=w3_plane[a, g][:],
+                    start=(a == 0), stop=(a == GROUPS - 1))
+            growth[u] = psum.tile([P, PASS], F32, name="growth", tag="growth", bufs=4)
+            for a in range(GROUPS):
+                nc.tensor.matmul_mx(
+                    out=growth[u][:], lhsT=x_codes[a][:, cols].bitcast(FP8X4), lhsT_scale=x_plane[a][:, cols],
+                    rhs=w2_codes[:, a, 2 * g * PASS:2 * (g + 1) * PASS].bitcast(FP4X4),
+                    rhs_scale=w2_plane[:, a, g * PASS:(g + 1) * PASS],
+                    start=(a == 0), stop=(a == GROUPS - 1))
+            turns = ring.tile([P, PACK, P], F32, name="turns", tag="turns")
+            nc.scalar.activation(turns[:], dealt(season), ACT.Abs, scale=1.0 / (2.0 * math.pi))
+            if u < 2:
+                whole = keep.tile([P, PACK, P], U32, name="whole", tag="upstream%d" % (6 + u), align_bytes=64)
+            else:
+                whole = ring.tile([P, PACK, P], U32, name="whole", tag="whole")
+            nc.scalar.activation(whole[:], turns[:], ACT.Copy, bias=0.25)
+            rest = ring.tile([P, PACK, P], F32, name="rest", tag="rest")
+            nc.vector.tensor_tensor(rest[:], turns[:], whole[:].bitcast(I32), ALU.subtract)
+            cosine[u] = ring.tile([P, PACK, P], F32, name="cosine", tag="cosine")
+            nc.scalar.activation(cosine[u][:], rest[:], ACT.Sin, scale=2.0 * math.pi, bias=0.5 * math.pi)
+
+        def turn(u):
+            product = ring.tile([P, PACK, P], F32, name="product", tag="product")
+            nc.vector.tensor_tensor(product[:], dealt(growth[u]), cosine[u][:], ALU.mult)
+            turned[u] = psum.tile([P, PACK, P], F32, name="turned", tag="turned", bufs=2)
+            for t in range(PACK):
+                nc.tensor.transpose(turned[u][:, t, :], product[:, t, :], ident[:])
+
+        def finish(u):
+            g, b = divmod(u, BLOCKS)
+            cols = slice(b * P, (b + 1) * P)
+            y = ring.tile([P, PACK, P], F32, name="y", tag="y", bufs=3)
+            for t in range(PACK):
+                nc.vector.scalar_tensor_tensor(y[:, t, :], upstream[g * PACK + t][:, cols], rs_t[:, g, t:t + 1],
+                                               turned[u][:, t, :], ALU.mult, ALU.add)
+            nc.sync.dma_start(out_rows[g][:, :, cols], y[:])
+            woven = ring.tile([P, P, PACK], BF16, name="y_woven", tag="woven", bufs=4, align_bytes=64)
+            nc.scalar.copy(woven[:].rearrange("p (c i) t -> p c t i", i=4),
+                           y[:].rearrange("p t (c i) -> p c t i", i=4))
+            nc.vector.quantize_mx(out=y_codes[g][:, cols].bitcast(FP8X4), scales=y_plane[:, g, cols],
+                                  in_=woven[:].rearrange("p c t -> p (c t)"))
+            if b % 2 == 1:
+                pair = slice((b - 1) * P, (b + 1) * P)
+                nc.sync.dma_start(out_words[g][:, pair], y_codes[g][:, pair])
+
+        units = GROUPS * BLOCKS
+        for step in range(units + 2):
+            if step < units:
+                multiply(step)
+            if step < 2:
+                fetch_upstream(6 + step, "upstream%d" % (6 + step))
+            if 1 <= step <= units:
+                turn(step - 1)
+            if step >= 2:
+                finish(step - 2)
+        for q in range(QUADS):
+            nc.sync.dma_start(out_2[:, 4 * q:4 * q + 4, :].rearrange("g r m -> r g m").bitcast(I32),
+                              y_plane[32 * q:32 * q + 4, :, :].bitcast(I32))

@@ -46,7 +46,7 @@ def tile_list_kelp_harvest_planner_kernel(
 
         def load_rowvec(source, name):
             tile = keep.tile([P, GROUPS, PACK], F32, name=name)
-            nc.gpsimd.dma_start(tile[:], source.rearrange("(g p t) -> p g t", g=GROUPS, t=PACK))
+            nc.sync.dma_start(tile[:], source.rearrange("(g p t) -> p g t", g=GROUPS, t=PACK))
             return tile
 
         w1_cols = w1_words.rearrange("a p c i -> p a (c i)").bitcast(I32)
@@ -57,7 +57,7 @@ def tile_list_kelp_harvest_planner_kernel(
         out_words = out_1.rearrange("g p m t -> g p (m t)").bitcast(I32)
 
         def load_w1(g):
-            tile = ring.tile([P, K_PASSES, PASS], I32, name="w1_raw", tag="w1_raw")
+            tile = ring.tile([P, K_PASSES, PASS], I32, name="w1_raw", tag="w1_raw", align_bytes=64)
             nc.sync.dma_start(tile[:], w1_cols[:, :, g * PASS:(g + 1) * PASS])
             return tile
 
@@ -82,67 +82,61 @@ def tile_list_kelp_harvest_planner_kernel(
         for q in range(QUADS):
             nc.scalar.dma_start(tab_plane[32 * q:32 * q + 4 * K_PASSES, :].bitcast(I32),
                                 tab_scales[:, 4 * q:4 * q + 4, :].bitcast(I32))
+        warm_out = keep.tile([P, 8], F32)
+        nc.scalar.activation(warm_out[:], warm[:], ACT.Silu)
         for q in range(QUADS):
             nc.gpsimd.dma_start(w1_plane_raw[32 * q:32 * q + 4 * K_PASSES, :].bitcast(I32),
                                 w1_scales[:, 4 * q:4 * q + 4, :].bitcast(I32))
-        warm_out = keep.tile([P, 8], F32)
-        nc.scalar.activation(warm_out[:], warm[:], ACT.Silu)
-        gain_t = load_rowvec(gain, "gain_t")
-        rs_t = load_rowvec(rs, "rs_t")
-        gx_t = load_rowvec(gx, "gx_t")
-        for q in range(QUADS):
-            nc.gpsimd.dma_start(w2_plane[32 * q:32 * q + 4, :, :].bitcast(I32),
-                                w2_scales[:, 4 * q:4 * q + 4, :].rearrange("a r n -> r a n").bitcast(I32))
         ident = keep.tile([P, P], F32)
         make_identity(nc, ident[:])
 
-        idx = load_list(offs, "idx")
-        idx2 = load_list(offs2, "idx2")
-        idx3 = load_list(offs3, "idx3")
-        idx4 = load_list(offs4, "idx4")
-        w1_raw = [load_w1(0)]
-        tab = []
-        for a in range(K_PASSES):
+        def load_tab(a):
             tile = ring.tile([P, T], I32, name="tab", tag="big", bufs=4)
             nc.sync.dma_start(tile[:], tab_words[a].rearrange("p c i -> p (c i)").bitcast(I32))
-            tab.append(tile)
+            return tile
+
+        idx = load_list(offs, "idx")
+        w1_raw = [load_w1(0)]
+        tab = [load_tab(a) for a in range(K_PASSES)]
+        gain_t = load_rowvec(gain, "gain_t")
+        idx2 = load_list(offs2, "idx2")
         pages = [load_page(0)]
-        wg_first = keep.tile([P, S], F32)
-        for q in range(QUADS):
-            nc.sync.dma_start(wg_first[32 * q:32 * q + 32, :], wgs_rows[:, 0, :])
-        wg_rest = keep.tile([P, PACK - 1, S], F32)
-        for q in range(QUADS):
-            nc.sync.dma_start(wg_rest[32 * q:32 * q + 32, :, :], wgs_rows[:, 1:PACK, :])
+        wg = []
+
+        def load_wg(first, count):
+            tile = keep.tile([P, count, S], F32, name="wg%d" % first)
+            for q in range(QUADS):
+                nc.sync.dma_start(tile[32 * q:32 * q + 32, :, :], wgs_rows[:, first:first + count, :])
+            wg.extend(tile[:, n, :] for n in range(count))
+
+        load_wg(0, 1)
         pages.append(load_page(1))
+        load_wg(1, 1)
         pages.append(load_page(2))
+        load_wg(2, 2)
         w1_raw.append(load_w1(1))
-        pages.append(load_page(3))
-        w3_raw = [load_w3(0)]
-        pages.append(load_page(4))
-        w3_raw.append(load_w3(1))
-        pages.append(load_page(5))
-        w3_raw.append(load_w3(2))
-        pages.append(load_page(6))
-        w3_raw.append(load_w3(3))
-        pages.append(load_page(7))
+        pages.extend(load_page(s) for s in range(3, SLICES))
+        w3_raw = [load_w3(q) for q in range(2 * GROUPS)]
         w2_codes = keep.tile([P, GROUPS, 2 * H], U8, align_bytes=64)
         nc.sync.dma_start(w2_codes[:].bitcast(I32), w2_words.rearrange("a p b -> p a b").bitcast(I32))
+        for q in range(QUADS):
+            nc.sync.dma_start(w2_plane[32 * q:32 * q + 4, :, :].bitcast(I32),
+                              w2_scales[:, 4 * q:4 * q + 4, :].rearrange("a r n -> r a n").bitcast(I32))
+        rs_t = load_rowvec(rs, "rs_t")
+        gx_t = load_rowvec(gx, "gx_t")
+        idx3 = load_list(offs3, "idx3")
+        idx4 = load_list(offs4, "idx4")
 
-        def wg(t):
-            return wg_first[:] if t == 0 else wg_rest[:, t - 1, :]
-
-        w1_dealt = {}
-
-        def deal_w1(g):
-            for a in range(K_PASSES):
-                tile = keep.tile([P, PACK, P], I32, name="w1_dealt%d_%d" % (g, a), align_bytes=64)
-                nc.vector.tensor_copy(tile[:].rearrange("p t m -> p m t"),
-                                      w1_raw[g][:, a, :].rearrange("p (m t) -> p m t", t=PACK))
-                w1_dealt[g, a] = tile
-
-        deal_w1(0)
-        w1_plane = keep.tile([P, GROUPS, PACK, P], U8, align_bytes=64)
-        nc.vector.tensor_copy(w1_plane[:], w1_plane_raw[:].rearrange("p (g m t) -> p g t m", g=GROUPS, t=PACK))
+        w1_dealt = []
+        for a in range(K_PASSES):
+            tile = keep.tile([P, PACK, P], I32, name="w1_dealt%d" % a, align_bytes=64)
+            nc.vector.tensor_copy(tile[:].rearrange("p (d e) m -> p d m e", e=2),
+                                  w1_raw[0][:, a, :].rearrange("p (m d e) -> p d m e", d=2, e=2))
+            w1_dealt.append(tile)
+        w1_plane_dealt = keep.tile([P, PACK, P], U8, align_bytes=64)
+        nc.vector.tensor_copy(w1_plane_dealt[:], w1_plane_raw[:, 0:PASS].rearrange("p (m t) -> p t m", t=PACK))
+        w1_plane_rest = keep.tile([P, PASS], U8, align_bytes=64)
+        nc.vector.tensor_copy(w1_plane_rest[:].bitcast(I32), w1_plane_raw[:, PASS:H].bitcast(I32))
         v_plane = keep.tile([P, S], U8, align_bytes=64)
         nc.vector.tensor_copy(v_plane[:], tab_plane[:].indirect(idx[:]))
         v_codes = []
@@ -151,46 +145,65 @@ def tile_list_kelp_harvest_planner_kernel(
             nc.vector.tensor_copy(tile[:].bitcast(U32), tab[a][:].bitcast(U32).indirect(idx[:]))
             v_codes.append(tile)
 
+        def dealt(bank):
+            return bank[:].rearrange("j (m t) -> j t m", t=PACK)
+
+        h_turned = keep.tile([P, BLOCKS, PACK, P], F32)
+
+        def multiply_turned():
+            for b in range(BLOCKS):
+                cols = slice(b * P, (b + 1) * P)
+                bank = psum.tile([P, PASS], F32, name="h_turned_bank", tag="growth", bufs=3)
+                for a in range(K_PASSES):
+                    nc.tensor.matmul_mx(
+                        out=bank[:], lhsT=v_codes[a][:, cols].bitcast(FP8X4), lhsT_scale=v_plane[4 * a:P, cols],
+                        rhs=w1_raw[1][:, a, :].bitcast(FP8X4), rhs_scale=w1_plane_rest[4 * a:P, :],
+                        start=(a == 0), stop=(a == K_PASSES - 1))
+                nc.scalar.copy(h_turned[:, b, :, :], dealt(bank))
+
         def put(s):
             g, t = divmod(s, PACK)
             bank = psum.tile([P, S], F32, name="h_bank", tag="early", bufs=2)
-            for a in range(K_PASSES):
-                nc.tensor.matmul_mx(
-                    out=bank[:], lhsT=w1_dealt[g, a][:, t, :].bitcast(FP8X4), lhsT_scale=w1_plane[4 * a:P, g, t, :],
-                    rhs=v_codes[a][:].bitcast(FP8X4), rhs_scale=v_plane[4 * a:P, :],
-                    start=(a == 0), stop=(a == K_PASSES - 1))
-            if s == SLICES - 1:
-                h = keep.tile([P, S], F32, name="h", tag="upstream4", align_bytes=64)
+            if g == 0:
+                for a in range(K_PASSES):
+                    nc.tensor.matmul_mx(
+                        out=bank[:], lhsT=w1_dealt[a][:, t, :].bitcast(FP8X4), lhsT_scale=w1_plane_dealt[4 * a:P, t, :],
+                        rhs=v_codes[a][:].bitcast(FP8X4), rhs_scale=v_plane[4 * a:P, :],
+                        start=(a == 0), stop=(a == K_PASSES - 1))
             else:
-                h = ring.tile([P, S], F32, name="h", tag="h", bufs=3)
+                for b in range(BLOCKS):
+                    nc.tensor.transpose(bank[:, b * P:(b + 1) * P], h_turned[:, b, t, :], ident[:])
+            h = ring.tile([P, S], F32, name="h", tag="h", bufs=3)
             nc.scalar.activation(h[:], bank[:], ACT.Copy, scale=gain_t[:, g, t:t + 1])
-            nc.vector.tensor_tensor(pages[s][:].indirect(idx2[:]), h[:], wg(t), ALU.mult)
+            nc.vector.tensor_tensor(pages[s][:].indirect(idx2[:]), h[:], wg[t], ALU.mult)
 
         x_codes = [keep.tile([P, PICKS], I32, name="x_codes%d" % g, align_bytes=64) for g in range(GROUPS)]
         x_plane = [keep.tile([P, PICKS], U8, name="x_plane%d" % g, align_bytes=64) for g in range(GROUPS)]
         x_woven = [keep.tile([P, PICKS, PACK], BF16, name="x_woven%d" % g, tag="x_woven%d" % g, align_bytes=64)
                    for g in range(GROUPS)]
 
-        def reread(s):
-            g, t = divmod(s, PACK)
-            picked = ring.tile([P, PICKS], F32, name="picked", tag="picked")
-            nc.vector.tensor_copy(picked[:], pages[s][:].indirect(idx3[:]))
-            bent = ring.tile([P, PICKS], F32, name="bent", tag="bent")
-            nc.scalar.activation(bent[:], picked[:], ACT.Tanh, scale=rs_t[:, g, t:t + 1])
-            pieces = BLOCKS if s == SLICES - 1 else 1
+        def reread(g):
+            picked = ring.tile([P, PACK, PICKS], F32, name="picked", tag="big", bufs=4)
+            x_rows = ring.tile([P, PACK, PICKS], BF16, name="x_rows", tag="x_rows")
+            for t in range(PACK):
+                nc.vector.tensor_copy(picked[:, t, :], pages[g * PACK + t][:].indirect(idx3[:]))
+                bent = ring.tile([P, PICKS], F32, name="bent", tag="bent")
+                nc.scalar.activation(bent[:], picked[:, t, :], ACT.Tanh, scale=rs_t[:, g, t:t + 1])
+                nc.scalar.activation(x_rows[:, t, :], bent[:], ACT.Copy, scale=gx_t[:, g, t:t + 1])
+            pieces = BLOCKS if g == GROUPS - 1 else 1
             width = PICKS // pieces
             for n in range(pieces):
                 cols = slice(n * width, (n + 1) * width)
-                nc.scalar.activation(x_woven[g][:, cols, t], bent[:, cols], ACT.Copy, scale=gx_t[:, g, t:t + 1])
-                if t == PACK - 1:
-                    nc.vector.quantize_mx(out=x_codes[g][:, cols].bitcast(FP8X4), scales=x_plane[g][:, cols],
-                                          in_=x_woven[g][:, cols, :].rearrange("p c t -> p (c t)"))
+                nc.scalar.copy(x_woven[g][:, cols, :].rearrange("p (c i) t -> p c t i", i=4),
+                               x_rows[:, :, cols].rearrange("p t (c i) -> p c t i", i=4))
+                nc.vector.quantize_mx(out=x_codes[g][:, cols].bitcast(FP8X4), scales=x_plane[g][:, cols],
+                                      in_=x_woven[g][:, cols, :].rearrange("p c t -> p (c t)"))
 
         w3_codes = {}
         w3_plane = {}
 
         def quantise_w3(q):
-            woven = ring.tile([P, PASS, PACK], BF16, name="w3_woven", tag="woven", bufs=4, align_bytes=64)
+            woven = ring.tile([P, PASS, PACK], BF16, name="w3_woven", tag="woven", bufs=3, align_bytes=64)
             for half in range(2):
                 cols = slice(half * PASS // 2, (half + 1) * PASS // 2)
                 nc.scalar.copy(woven[:, cols, :].rearrange("p (c i) t -> p c t i", i=4),
@@ -203,65 +216,63 @@ def tile_list_kelp_harvest_planner_kernel(
 
         upstream = {}
 
-        def fetch_upstream(s, tag):
-            upstream[s] = keep.tile([P, PICKS], F32, name="upstream%d" % s, tag=tag, align_bytes=64)
-            nc.vector.tensor_copy(upstream[s][:], pages[s][:].indirect(idx4[:]))
+        def fetch_upstream(first, count, tag):
+            tile = keep.tile([P, count, PICKS], F32, name="upstream%d" % first, tag=tag, align_bytes=64)
+            for n in range(count):
+                upstream[first + n] = tile[:, n, :]
+                nc.vector.tensor_copy(tile[:, n, :], pages[first + n][:].indirect(idx4[:]))
 
         for s in range(SLICES):
             if s == PACK - 1:
-                deal_w1(1)
+                multiply_turned()
             put(s)
-            if s > 0:
-                reread(s - 1)
-            if 0 < s <= PACK:
-                fetch_upstream(s - 1, "upstream%d" % (s - 1))
-            if s >= PACK:
-                quantise_w3(s - PACK)
-        reread(SLICES - 1)
-        fetch_upstream(4, "upstream4")
-        fetch_upstream(5, "x_woven1")
+        for q in range(2 * GROUPS):
+            quantise_w3(q)
+        for g in range(GROUPS):
+            reread(g)
+        fetch_upstream(0, PACK, "upstream0")
+        fetch_upstream(4, 2, "x_woven1")
 
         y_codes = [keep.tile([P, PICKS], I32, name="y_codes%d" % g, align_bytes=64) for g in range(GROUPS)]
         y_plane = keep.tile([P, GROUPS, PICKS], U8, align_bytes=64)
-        cosine = {}
-        growth = {}
-        turned = {}
+        turns, whole, cosine, growth, turned, y_woven = {}, {}, {}, {}, {}, {}
 
-        def dealt(bank):
-            return bank[:].rearrange("j (m t) -> j t m", t=PACK)
+        def multiply(bank, u, codes, plane):
+            cols = slice(u % BLOCKS * P, (u % BLOCKS + 1) * P)
+            for a in range(GROUPS):
+                nc.tensor.matmul_mx(
+                    out=bank[:], lhsT=x_codes[a][:, cols].bitcast(FP8X4), lhsT_scale=x_plane[a][:, cols],
+                    rhs=codes[a], rhs_scale=plane[a], start=(a == 0), stop=(a == GROUPS - 1))
 
-        def multiply(u):
-            g, b = divmod(u, BLOCKS)
-            cols = slice(b * P, (b + 1) * P)
+        def count_turns(u):
+            g = u // BLOCKS
             season = psum.tile([P, PASS], F32, name="season", tag="early", bufs=2)
-            for a in range(GROUPS):
-                nc.tensor.matmul_mx(
-                    out=season[:], lhsT=x_codes[a][:, cols].bitcast(FP8X4), lhsT_scale=x_plane[a][:, cols],
-                    rhs=w3_codes[a, g][:].bitcast(FP8X4), rhs_scale=w3_plane[a, g][:],
-                    start=(a == 0), stop=(a == GROUPS - 1))
-            growth[u] = psum.tile([P, PASS], F32, name="growth", tag="growth", bufs=4)
-            for a in range(GROUPS):
-                nc.tensor.matmul_mx(
-                    out=growth[u][:], lhsT=x_codes[a][:, cols].bitcast(FP8X4), lhsT_scale=x_plane[a][:, cols],
-                    rhs=w2_codes[:, a, 2 * g * PASS:2 * (g + 1) * PASS].bitcast(FP4X4),
-                    rhs_scale=w2_plane[:, a, g * PASS:(g + 1) * PASS],
-                    start=(a == 0), stop=(a == GROUPS - 1))
-            turns = ring.tile([P, PACK, P], F32, name="turns", tag="turns")
-            nc.scalar.activation(turns[:], dealt(season), ACT.Abs, scale=1.0 / (2.0 * math.pi))
+            multiply(season, u, [w3_codes[a, g][:].bitcast(FP8X4) for a in range(GROUPS)],
+                     [w3_plane[a, g][:] for a in range(GROUPS)])
+            turns[u] = ring.tile([P, PACK, P], F32, name="turns", tag="turns", bufs=3)
+            nc.scalar.activation(turns[u][:], dealt(season), ACT.Abs, scale=1.0 / (2.0 * math.pi))
             if u < 2:
-                whole = keep.tile([P, PACK, P], U32, name="whole", tag="upstream%d" % (6 + u), align_bytes=64)
+                whole[u] = keep.tile([P, PACK, P], U32, name="whole", tag="upstream%d" % (6 + u), align_bytes=64)
             else:
-                whole = ring.tile([P, PACK, P], U32, name="whole", tag="whole")
-            nc.scalar.activation(whole[:], turns[:], ACT.Copy, bias=0.25)
+                whole[u] = ring.tile([P, PACK, P], U32, name="whole", tag="whole", bufs=3)
+            nc.scalar.activation(whole[u][:], turns[u][:], ACT.Copy, bias=0.25)
+
+        def take_cosine(u):
+            g = u // BLOCKS
             rest = ring.tile([P, PACK, P], F32, name="rest", tag="rest")
-            nc.vector.tensor_tensor(rest[:], turns[:], whole[:].bitcast(I32), ALU.subtract)
-            cosine[u] = ring.tile([P, PACK, P], F32, name="cosine", tag="cosine")
+            nc.vector.tensor_tensor(rest[:], turns[u][:], whole[u][:].bitcast(I32), ALU.subtract)
+            if u < 2:
+                fetch_upstream(6 + u, 1, "upstream%d" % (6 + u))
+            cosine[u] = ring.tile([P, PACK, P], F32, name="cosine", tag="cosine", bufs=3)
             nc.scalar.activation(cosine[u][:], rest[:], ACT.Sin, scale=2.0 * math.pi, bias=0.5 * math.pi)
+            growth[u] = psum.tile([P, PASS], F32, name="growth", tag="growth", bufs=3)
+            multiply(growth[u], u, [w2_codes[:, a, 2 * g * PASS:2 * (g + 1) * PASS].bitcast(FP4X4) for a in range(GROUPS)],
+                     [w2_plane[:, a, g * PASS:(g + 1) * PASS] for a in range(GROUPS)])
 
         def turn(u):
             product = ring.tile([P, PACK, P], F32, name="product", tag="product")
             nc.vector.tensor_tensor(product[:], dealt(growth[u]), cosine[u][:], ALU.mult)
-            turned[u] = psum.tile([P, PACK, P], F32, name="turned", tag="turned", bufs=2)
+            turned[u] = psum.tile([P, PACK, P], F32, name="turned", tag="turned", bufs=3)
             for t in range(PACK):
                 nc.tensor.transpose(turned[u][:, t, :], product[:, t, :], ident[:])
 
@@ -273,25 +284,25 @@ def tile_list_kelp_harvest_planner_kernel(
                 nc.vector.scalar_tensor_tensor(y[:, t, :], upstream[g * PACK + t][:, cols], rs_t[:, g, t:t + 1],
                                                turned[u][:, t, :], ALU.mult, ALU.add)
             nc.sync.dma_start(out_rows[g][:, :, cols], y[:])
-            woven = ring.tile([P, P, PACK], BF16, name="y_woven", tag="woven", bufs=4, align_bytes=64)
-            nc.scalar.copy(woven[:].rearrange("p (c i) t -> p c t i", i=4),
+            y_woven[u] = ring.tile([P, P, PACK], BF16, name="y_woven", tag="woven", bufs=3, align_bytes=64)
+            nc.scalar.copy(y_woven[u][:].rearrange("p (c i) t -> p c t i", i=4),
                            y[:].rearrange("p t (c i) -> p c t i", i=4))
+
+        def quantise_y(u):
+            g, b = divmod(u, BLOCKS)
+            cols = slice(b * P, (b + 1) * P)
             nc.vector.quantize_mx(out=y_codes[g][:, cols].bitcast(FP8X4), scales=y_plane[:, g, cols],
-                                  in_=woven[:].rearrange("p c t -> p (c t)"))
+                                  in_=y_woven[u][:].rearrange("p c t -> p (c t)"))
             if b % 2 == 1:
                 pair = slice((b - 1) * P, (b + 1) * P)
                 nc.sync.dma_start(out_words[g][:, pair], y_codes[g][:, pair])
 
+        stages = [count_turns, take_cosine, turn, finish, quantise_y]
         units = GROUPS * BLOCKS
-        for step in range(units + 2):
-            if step < units:
-                multiply(step)
-            if step < 2:
-                fetch_upstream(6 + step, "upstream%d" % (6 + step))
-            if 1 <= step <= units:
-                turn(step - 1)
-            if step >= 2:
-                finish(step - 2)
+        for step in range(units + len(stages) - 1):
+            for depth, stage in enumerate(stages):
+                if 0 <= step - depth < units:
+                    stage(step - depth)
         for q in range(QUADS):
             nc.sync.dma_start(out_2[:, 4 * q:4 * q + 4, :].rearrange("g r m -> r g m").bitcast(I32),
                               y_plane[32 * q:32 * q + 4, :, :].bitcast(I32))

@@ -145,8 +145,11 @@ def tile_list_kelp_harvest_planner_kernel(
             nc.vector.tensor_copy(tile[:].bitcast(U32), tab[a][:].bitcast(U32).indirect(idx[:]))
             v_codes.append(tile)
 
-        def dealt(bank):
-            return bank[:].rearrange("j (m t) -> j t m", t=PACK)
+        def pairs_of(bank):
+            return bank[:].rearrange("j (m d e) -> j d m e", d=2, e=2)
+
+        def dealt(rows):
+            return rows.rearrange("j (d e) m -> j d m e", e=2)
 
         h_turned = keep.tile([P, BLOCKS, PACK, P], F32)
 
@@ -159,7 +162,7 @@ def tile_list_kelp_harvest_planner_kernel(
                         out=bank[:], lhsT=v_codes[a][:, cols].bitcast(FP8X4), lhsT_scale=v_plane[4 * a:P, cols],
                         rhs=w1_raw[1][:, a, :].bitcast(FP8X4), rhs_scale=w1_plane_rest[4 * a:P, :],
                         start=(a == 0), stop=(a == K_PASSES - 1))
-                nc.scalar.copy(h_turned[:, b, :, :], dealt(bank))
+                nc.scalar.copy(dealt(h_turned[:, b, :, :]), pairs_of(bank))
 
         def put(s):
             g, t = divmod(s, PACK)
@@ -194,8 +197,8 @@ def tile_list_kelp_harvest_planner_kernel(
             width = PICKS // pieces
             for n in range(pieces):
                 cols = slice(n * width, (n + 1) * width)
-                nc.scalar.copy(x_woven[g][:, cols, :].rearrange("p (c i) t -> p c t i", i=4),
-                               x_rows[:, :, cols].rearrange("p t (c i) -> p c t i", i=4))
+                nc.scalar.copy(x_woven[g][:, cols, :].rearrange("p (c i) t -> p c t i", i=2),
+                               x_rows[:, :, cols].rearrange("p t (c i) -> p c t i", i=2))
                 nc.vector.quantize_mx(out=x_codes[g][:, cols].bitcast(FP8X4), scales=x_plane[g][:, cols],
                                       in_=x_woven[g][:, cols, :].rearrange("p c t -> p (c t)"))
 
@@ -206,8 +209,8 @@ def tile_list_kelp_harvest_planner_kernel(
             woven = ring.tile([P, PASS, PACK], BF16, name="w3_woven", tag="woven", bufs=3, align_bytes=64)
             for half in range(2):
                 cols = slice(half * PASS // 2, (half + 1) * PASS // 2)
-                nc.scalar.copy(woven[:, cols, :].rearrange("p (c i) t -> p c t i", i=4),
-                               w3_raw[q][:, :, cols].rearrange("p t (c i) -> p c t i", i=4))
+                nc.scalar.copy(woven[:, cols, :].rearrange("p (c i) t -> p c t i", i=2),
+                               w3_raw[q][:, :, cols].rearrange("p t (c i) -> p c t i", i=2))
             key = divmod(q, 2)
             w3_codes[key] = keep.tile([P, PASS], I32, name="w3_codes%d" % q, align_bytes=64)
             w3_plane[key] = keep.tile([P, PASS], U8, name="w3_plane%d" % q, align_bytes=64)
@@ -249,21 +252,21 @@ def tile_list_kelp_harvest_planner_kernel(
             season = psum.tile([P, PASS], F32, name="season", tag="early", bufs=2)
             multiply(season, u, [w3_codes[a, g][:].bitcast(FP8X4) for a in range(GROUPS)],
                      [w3_plane[a, g][:] for a in range(GROUPS)])
-            turns[u] = ring.tile([P, PACK, P], F32, name="turns", tag="turns", bufs=3)
-            nc.scalar.activation(turns[u][:], dealt(season), ACT.Abs, scale=1.0 / (2.0 * math.pi))
+            turns[u] = ring.tile([P, 2, P, 2], F32, name="turns", tag="turns", bufs=3)
+            nc.scalar.activation(turns[u][:], pairs_of(season), ACT.Abs, scale=1.0 / (2.0 * math.pi))
             if u < 2:
-                whole[u] = keep.tile([P, PACK, P], U32, name="whole", tag="upstream%d" % (6 + u), align_bytes=64)
+                whole[u] = keep.tile([P, 2, P, 2], U32, name="whole", tag="upstream%d" % (6 + u), align_bytes=64)
             else:
-                whole[u] = ring.tile([P, PACK, P], U32, name="whole", tag="whole", bufs=3)
+                whole[u] = ring.tile([P, 2, P, 2], U32, name="whole", tag="whole", bufs=3)
             nc.scalar.activation(whole[u][:], turns[u][:], ACT.Copy, bias=0.25)
 
         def take_cosine(u):
             g = u // BLOCKS
-            rest = ring.tile([P, PACK, P], F32, name="rest", tag="rest")
+            rest = ring.tile([P, 2, P, 2], F32, name="rest", tag="rest")
             nc.vector.tensor_tensor(rest[:], turns[u][:], whole[u][:].bitcast(I32), ALU.subtract)
             if u < 2:
                 fetch_upstream(6 + u, 1, "upstream%d" % (6 + u))
-            cosine[u] = ring.tile([P, PACK, P], F32, name="cosine", tag="cosine", bufs=3)
+            cosine[u] = ring.tile([P, 2, P, 2], F32, name="cosine", tag="cosine", bufs=3)
             nc.scalar.activation(cosine[u][:], rest[:], ACT.Sin, scale=2.0 * math.pi, bias=0.5 * math.pi)
             growth[u] = psum.tile([P, PASS], F32, name="growth", tag="growth", bufs=3)
             multiply(growth[u], u, [w2_codes[:, a, 2 * g * PASS:2 * (g + 1) * PASS].bitcast(FP4X4) for a in range(GROUPS)],
@@ -271,7 +274,7 @@ def tile_list_kelp_harvest_planner_kernel(
 
         def turn(u):
             product = ring.tile([P, PACK, P], F32, name="product", tag="product")
-            nc.vector.tensor_tensor(product[:], dealt(growth[u]), cosine[u][:], ALU.mult)
+            nc.vector.tensor_tensor(dealt(product[:]), pairs_of(growth[u]), cosine[u][:], ALU.mult)
             turned[u] = psum.tile([P, PACK, P], F32, name="turned", tag="turned", bufs=3)
             for t in range(PACK):
                 nc.tensor.transpose(turned[u][:, t, :], product[:, t, :], ident[:])
@@ -285,8 +288,8 @@ def tile_list_kelp_harvest_planner_kernel(
                                                turned[u][:, t, :], ALU.mult, ALU.add)
             nc.sync.dma_start(out_rows[g][:, :, cols], y[:])
             y_woven[u] = ring.tile([P, P, PACK], BF16, name="y_woven", tag="woven", bufs=3, align_bytes=64)
-            nc.scalar.copy(y_woven[u][:].rearrange("p (c i) t -> p c t i", i=4),
-                           y[:].rearrange("p t (c i) -> p c t i", i=4))
+            nc.scalar.copy(y_woven[u][:].rearrange("p (c i) t -> p c t i", i=2),
+                           y[:].rearrange("p t (c i) -> p c t i", i=2))
 
         def quantise_y(u):
             g, b = divmod(u, BLOCKS)

@@ -46,7 +46,7 @@ def tile_list_kelp_harvest_planner_kernel(
 
         def load_rowvec(source, name):
             tile = keep.tile([P, GROUPS, PACK], F32, name=name)
-            nc.sync.dma_start(tile[:], source.rearrange("(g p t) -> p g t", g=GROUPS, t=PACK))
+            nc.gpsimd.dma_start(tile[:], source.rearrange("(g p t) -> p g t", g=GROUPS, t=PACK))
             return tile
 
         w1_cols = w1_words.rearrange("a p c i -> p a (c i)").bitcast(I32)
@@ -87,6 +87,9 @@ def tile_list_kelp_harvest_planner_kernel(
         for q in range(QUADS):
             nc.gpsimd.dma_start(w1_plane_raw[32 * q:32 * q + 4 * K_PASSES, :].bitcast(I32),
                                 w1_scales[:, 4 * q:4 * q + 4, :].bitcast(I32))
+        gain_t = load_rowvec(gain, "gain_t")
+        rs_t = load_rowvec(rs, "rs_t")
+        gx_t = load_rowvec(gx, "gx_t")
         ident = keep.tile([P, P], F32)
         make_identity(nc, ident[:])
 
@@ -95,10 +98,10 @@ def tile_list_kelp_harvest_planner_kernel(
             nc.sync.dma_start(tile[:], tab_words[a].rearrange("p c i -> p (c i)").bitcast(I32))
             return tile
 
-        idx = load_list(offs, "idx")
         w1_raw = [load_w1(0)]
-        tab = [load_tab(a) for a in range(K_PASSES)]
-        gain_t = load_rowvec(gain, "gain_t")
+        tab = [load_tab(0)]
+        idx = load_list(offs, "idx")
+        tab.extend(load_tab(a) for a in range(1, K_PASSES))
         idx2 = load_list(offs2, "idx2")
         pages = [load_page(0)]
         wg = []
@@ -115,16 +118,15 @@ def tile_list_kelp_harvest_planner_kernel(
         pages.append(load_page(2))
         load_wg(2, 2)
         w1_raw.append(load_w1(1))
-        pages.extend(load_page(s) for s in range(3, SLICES))
+        pages.append(load_page(3))
+        idx3 = load_list(offs3, "idx3")
+        pages.extend(load_page(s) for s in range(PACK, SLICES))
         w3_raw = [load_w3(q) for q in range(2 * GROUPS)]
         w2_codes = keep.tile([P, GROUPS, 2 * H], U8, align_bytes=64)
         nc.sync.dma_start(w2_codes[:].bitcast(I32), w2_words.rearrange("a p b -> p a b").bitcast(I32))
         for q in range(QUADS):
             nc.sync.dma_start(w2_plane[32 * q:32 * q + 4, :, :].bitcast(I32),
                               w2_scales[:, 4 * q:4 * q + 4, :].rearrange("a r n -> r a n").bitcast(I32))
-        rs_t = load_rowvec(rs, "rs_t")
-        gx_t = load_rowvec(gx, "gx_t")
-        idx3 = load_list(offs3, "idx3")
         idx4 = load_list(offs4, "idx4")
 
         w1_dealt = []
@@ -186,7 +188,10 @@ def tile_list_kelp_harvest_planner_kernel(
                    for g in range(GROUPS)]
 
         def reread(g):
-            picked = ring.tile([P, PACK, PICKS], F32, name="picked", tag="big", bufs=4)
+            if g == 0:
+                picked = keep.tile([P, PACK, PICKS], F32, name="picked")
+            else:
+                picked = ring.tile([P, PACK, PICKS], F32, name="picked", tag="big", bufs=4)
             x_rows = ring.tile([P, PACK, PICKS], BF16, name="x_rows", tag="x_rows")
             for t in range(PACK):
                 nc.vector.tensor_copy(picked[:, t, :], pages[g * PACK + t][:].indirect(idx3[:]))
@@ -229,12 +234,12 @@ def tile_list_kelp_harvest_planner_kernel(
             if s == PACK - 1:
                 multiply_turned()
             put(s)
+        reread(0)
         for q in range(2 * GROUPS):
             quantise_w3(q)
-        for g in range(GROUPS):
-            reread(g)
-        fetch_upstream(0, PACK, "upstream0")
-        fetch_upstream(4, 2, "x_woven1")
+        reread(1)
+        fetch_upstream(0, 1, "upstream0")
+        fetch_upstream(1, 2, "x_woven1")
 
         y_codes = [keep.tile([P, PICKS], I32, name="y_codes%d" % g, align_bytes=64) for g in range(GROUPS)]
         y_plane = keep.tile([P, GROUPS, PICKS], U8, align_bytes=64)
@@ -254,8 +259,8 @@ def tile_list_kelp_harvest_planner_kernel(
                      [w3_plane[a, g][:] for a in range(GROUPS)])
             turns[u] = ring.tile([P, 2, P, 2], F32, name="turns", tag="turns", bufs=3)
             nc.scalar.activation(turns[u][:], pairs_of(season), ACT.Abs, scale=1.0 / (2.0 * math.pi))
-            if u < 2:
-                whole[u] = keep.tile([P, 2, P, 2], U32, name="whole", tag="upstream%d" % (6 + u), align_bytes=64)
+            if u < 5:
+                whole[u] = keep.tile([P, 2, P, 2], U32, name="whole", tag="upstream%d" % (3 + u), align_bytes=64)
             else:
                 whole[u] = ring.tile([P, 2, P, 2], U32, name="whole", tag="whole", bufs=3)
             nc.scalar.activation(whole[u][:], turns[u][:], ACT.Copy, bias=0.25)
@@ -264,8 +269,8 @@ def tile_list_kelp_harvest_planner_kernel(
             g = u // BLOCKS
             rest = ring.tile([P, 2, P, 2], F32, name="rest", tag="rest")
             nc.vector.tensor_tensor(rest[:], turns[u][:], whole[u][:].bitcast(I32), ALU.subtract)
-            if u < 2:
-                fetch_upstream(6 + u, 1, "upstream%d" % (6 + u))
+            if u < 5:
+                fetch_upstream(3 + u, 1, "upstream%d" % (3 + u))
             cosine[u] = ring.tile([P, 2, P, 2], F32, name="cosine", tag="cosine", bufs=3)
             nc.scalar.activation(cosine[u][:], rest[:], ACT.Sin, scale=2.0 * math.pi, bias=0.5 * math.pi)
             growth[u] = psum.tile([P, PASS], F32, name="growth", tag="growth", bufs=3)
@@ -307,5 +312,5 @@ def tile_list_kelp_harvest_planner_kernel(
                 if 0 <= step - depth < units:
                     stage(step - depth)
         for q in range(QUADS):
-            nc.sync.dma_start(out_2[:, 4 * q:4 * q + 4, :].rearrange("g r m -> r g m").bitcast(I32),
+            nc.scalar.dma_start(out_2[:, 4 * q:4 * q + 4, :].rearrange("g r m -> r g m").bitcast(I32),
                               y_plane[32 * q:32 * q + 4, :, :].bitcast(I32))

@@ -26,6 +26,9 @@ K_PASSES = K // PASS
 GROUPS = H // PASS
 SLICES = GROUPS * PACK
 BLOCKS = PICKS // P
+UNITS = GROUPS * BLOCKS
+LIST_COLS = S // 16
+EARLY_UPSTREAM = 3
 
 
 def tile_list_kelp_harvest_planner_kernel(
@@ -39,16 +42,6 @@ def tile_list_kelp_harvest_planner_kernel(
         ring = ctx.enter_context(tc.tile_pool(name="ring", bufs=2))
         psum = ctx.enter_context(tc.psum_pool(name="psum", bufs=1))
 
-        def load_list(source, name):
-            tile = lists.tile([P, S // 16], U16, name=name)
-            nc.sync.dma_start(tile[:], source)
-            return tile
-
-        def load_rowvec(source, name):
-            tile = keep.tile([P, GROUPS, PACK], F32, name=name)
-            nc.gpsimd.dma_start(tile[:], source.rearrange("(g p t) -> p g t", g=GROUPS, t=PACK))
-            return tile
-
         w1_cols = w1_words.rearrange("a p c i -> p a (c i)").bitcast(I32)
         page_rows = page0.rearrange("(g p t) c -> g t p c", g=GROUPS, t=PACK)
         wgs_rows = wgs.rearrange("(m t) s -> m t s", t=PACK)
@@ -56,9 +49,29 @@ def tile_list_kelp_harvest_planner_kernel(
         out_rows = out_0.rearrange("(g p t) j -> g p t j", g=GROUPS, t=PACK)
         out_words = out_1.rearrange("g p m t -> g p (m t)").bitcast(I32)
 
+        def load_list(source, name):
+            tile = lists.tile([P, LIST_COLS], U16, name=name)
+            nc.sync.dma_start(tile[:], source)
+            return tile
+
+        def load_by_slice(source, name):
+            tile = keep.tile([P, GROUPS, PACK], F32, name=name)
+            nc.gpsimd.dma_start(tile[:], source.rearrange("(g p t) -> p g t", g=GROUPS, t=PACK))
+            return tile
+
         def load_w1(g):
             tile = ring.tile([P, K_PASSES, PASS], I32, name="w1_raw", tag="w1_raw", align_bytes=64)
             nc.sync.dma_start(tile[:], w1_cols[:, :, g * PASS:(g + 1) * PASS])
+            return tile
+
+        def load_tab(a):
+            tile = ring.tile([P, T], I32, name="tab", tag="large", bufs=4)
+            nc.sync.dma_start(tile[:], tab_words[a].rearrange("p c i -> p (c i)").bitcast(I32))
+            return tile
+
+        def load_w3(q):
+            tile = ring.tile([P, PACK, PASS], F32, name="w3_raw", tag="large", bufs=4)
+            nc.sync.dma_start(tile[:], w3_rows[q // 2][:, :, (q % 2) * PASS:(q % 2 + 1) * PASS])
             return tile
 
         def load_page(s):
@@ -66,44 +79,6 @@ def tile_list_kelp_harvest_planner_kernel(
             nc.sync.dma_start(tile[:], page_rows[s // PACK, s % PACK])
             return tile
 
-        def load_w3(q):
-            tile = ring.tile([P, PACK, PASS], F32, name="w3_raw", tag="big", bufs=4)
-            nc.sync.dma_start(tile[:], w3_rows[q // 2][:, :, (q % 2) * PASS:(q % 2 + 1) * PASS])
-            return tile
-
-        tab_plane = keep.tile([P, T], U8, tag="v_codes2", align_bytes=64)
-        w1_plane_raw = keep.tile([P, H], U8, tag="v_codes1", align_bytes=64)
-        w2_plane = keep.tile([P, GROUPS, H], U8, align_bytes=64)
-        warm = keep.tile([P, 8], F32)
-        nc.gpsimd.memset(tab_plane[:].bitcast(I32), 0)
-        nc.gpsimd.memset(w1_plane_raw[:].bitcast(I32), 0)
-        nc.vector.memset(warm[:], 0.0)
-        nc.vector.memset(w2_plane[:].bitcast(I32), 0)
-        for q in range(QUADS):
-            nc.scalar.dma_start(tab_plane[32 * q:32 * q + 4 * K_PASSES, :].bitcast(I32),
-                                tab_scales[:, 4 * q:4 * q + 4, :].bitcast(I32))
-        warm_out = keep.tile([P, 8], F32)
-        nc.scalar.activation(warm_out[:], warm[:], ACT.Silu)
-        for q in range(QUADS):
-            nc.gpsimd.dma_start(w1_plane_raw[32 * q:32 * q + 4 * K_PASSES, :].bitcast(I32),
-                                w1_scales[:, 4 * q:4 * q + 4, :].bitcast(I32))
-        gain_t = load_rowvec(gain, "gain_t")
-        rs_t = load_rowvec(rs, "rs_t")
-        gx_t = load_rowvec(gx, "gx_t")
-        ident = keep.tile([P, P], F32)
-        make_identity(nc, ident[:])
-
-        def load_tab(a):
-            tile = ring.tile([P, T], I32, name="tab", tag="big", bufs=4)
-            nc.sync.dma_start(tile[:], tab_words[a].rearrange("p c i -> p (c i)").bitcast(I32))
-            return tile
-
-        w1_raw = [load_w1(0)]
-        tab = [load_tab(0)]
-        idx = load_list(offs, "idx")
-        tab.extend(load_tab(a) for a in range(1, K_PASSES))
-        idx2 = load_list(offs2, "idx2")
-        pages = [load_page(0)]
         wg = []
 
         def load_wg(first, count):
@@ -112,6 +87,34 @@ def tile_list_kelp_harvest_planner_kernel(
                 nc.sync.dma_start(tile[32 * q:32 * q + 32, :, :], wgs_rows[:, first:first + count, :])
             wg.extend(tile[:, n, :] for n in range(count))
 
+        tab_plane = keep.tile([P, T], U8, tag="v_codes2", align_bytes=64)
+        w1_plane_raw = keep.tile([P, H], U8, tag="v_codes1", align_bytes=64)
+        w2_plane = keep.tile([P, GROUPS, H], U8, align_bytes=64)
+        silu_input = keep.tile([P, 1], F32)
+        nc.gpsimd.memset(w1_plane_raw[:].bitcast(I32), 0)
+        nc.gpsimd.memset(tab_plane[:].bitcast(I32), 0)
+        nc.vector.memset(silu_input[:], 0.0)
+        nc.vector.memset(w2_plane[:].bitcast(I32), 0)
+        for q in range(QUADS):
+            nc.gpsimd.dma_start(tab_plane[32 * q:32 * q + 4 * K_PASSES, :].bitcast(I32),
+                                tab_scales[:, 4 * q:4 * q + 4, :].bitcast(I32))
+        for q in range(QUADS):
+            nc.scalar.dma_start(w1_plane_raw[32 * q:32 * q + 4 * K_PASSES, :].bitcast(I32),
+                                w1_scales[:, 4 * q:4 * q + 4, :].bitcast(I32))
+        zero_bias = keep.tile([P, 1], F32)
+        nc.scalar.activation(zero_bias[:], silu_input[:], ACT.Silu)
+        gain_t = load_by_slice(gain, "gain_t")
+        rs_t = load_by_slice(rs, "rs_t")
+        gx_t = load_by_slice(gx, "gx_t")
+        ident = keep.tile([P, P], F32)
+        make_identity(nc, ident[:])
+
+        w1_raw = [load_w1(0)]
+        tab = [load_tab(0)]
+        idx = load_list(offs, "idx")
+        tab.extend(load_tab(a) for a in range(1, K_PASSES))
+        idx2 = load_list(offs2, "idx2")
+        pages = [load_page(0)]
         load_wg(0, 1)
         pages.append(load_page(1))
         load_wg(1, 1)
@@ -129,11 +132,22 @@ def tile_list_kelp_harvest_planner_kernel(
                               w2_scales[:, 4 * q:4 * q + 4, :].rearrange("a r n -> r a n").bitcast(I32))
         idx4 = load_list(offs4, "idx4")
 
+        def pairs_of(columns):
+            return columns.rearrange("p (m d e) -> p d m e", d=2, e=2)
+
+        def dealt(rows):
+            return rows.rearrange("p (d e) m -> p d m e", e=2)
+
+        def weave(woven, rows):
+            nc.scalar.copy(woven.rearrange("p (c i) t -> p c t i", i=2), rows.rearrange("p t (c i) -> p c t i", i=2))
+
+        def quantise(codes, plane, woven):
+            nc.vector.quantize_mx(out=codes.bitcast(FP8X4), scales=plane, in_=woven.rearrange("p c t -> p (c t)"))
+
         w1_dealt = []
         for a in range(K_PASSES):
             tile = keep.tile([P, PACK, P], I32, name="w1_dealt%d" % a, align_bytes=64)
-            nc.vector.tensor_copy(tile[:].rearrange("p (d e) m -> p d m e", e=2),
-                                  w1_raw[0][:, a, :].rearrange("p (m d e) -> p d m e", d=2, e=2))
+            nc.vector.tensor_copy(dealt(tile[:]), pairs_of(w1_raw[0][:, a, :]))
             w1_dealt.append(tile)
         w1_plane_dealt = keep.tile([P, PACK, P], U8, align_bytes=64)
         nc.vector.tensor_copy(w1_plane_dealt[:], w1_plane_raw[:, 0:PASS].rearrange("p (m t) -> p t m", t=PACK))
@@ -141,17 +155,16 @@ def tile_list_kelp_harvest_planner_kernel(
         nc.vector.tensor_copy(w1_plane_rest[:].bitcast(I32), w1_plane_raw[:, PASS:H].bitcast(I32))
         v_plane = keep.tile([P, S], U8, align_bytes=64)
         nc.vector.tensor_copy(v_plane[:], tab_plane[:].indirect(idx[:]))
+
+        whole_list = [(slice(0, S), slice(0, LIST_COLS))]
+        halves = [(slice(n * S // 2, (n + 1) * S // 2), slice(n * LIST_COLS // 2, (n + 1) * LIST_COLS // 2))
+                  for n in range(2)]
         v_codes = []
         for a in range(K_PASSES):
             tile = keep.tile([P, S], I32, name="v_codes%d" % a, tag="v_codes%d" % a, align_bytes=64)
-            nc.vector.tensor_copy(tile[:].bitcast(U32), tab[a][:].bitcast(U32).indirect(idx[:]))
+            for cols, entries in (halves if a == K_PASSES - 1 else whole_list):
+                nc.vector.tensor_copy(tile[:, cols].bitcast(U32), tab[a][:].bitcast(U32).indirect(idx[:, entries]))
             v_codes.append(tile)
-
-        def pairs_of(bank):
-            return bank[:].rearrange("j (m d e) -> j d m e", d=2, e=2)
-
-        def dealt(rows):
-            return rows.rearrange("j (d e) m -> j d m e", e=2)
 
         h_turned = keep.tile([P, BLOCKS, PACK, P], F32)
 
@@ -164,23 +177,25 @@ def tile_list_kelp_harvest_planner_kernel(
                         out=bank[:], lhsT=v_codes[a][:, cols].bitcast(FP8X4), lhsT_scale=v_plane[4 * a:P, cols],
                         rhs=w1_raw[1][:, a, :].bitcast(FP8X4), rhs_scale=w1_plane_rest[4 * a:P, :],
                         start=(a == 0), stop=(a == K_PASSES - 1))
-                nc.scalar.copy(dealt(h_turned[:, b, :, :]), pairs_of(bank))
+                nc.scalar.copy(dealt(h_turned[:, b, :, :]), pairs_of(bank[:]))
 
         def put(s):
             g, t = divmod(s, PACK)
-            bank = psum.tile([P, S], F32, name="h_bank", tag="early", bufs=2)
-            if g == 0:
-                for a in range(K_PASSES):
-                    nc.tensor.matmul_mx(
-                        out=bank[:], lhsT=w1_dealt[a][:, t, :].bitcast(FP8X4), lhsT_scale=w1_plane_dealt[4 * a:P, t, :],
-                        rhs=v_codes[a][:].bitcast(FP8X4), rhs_scale=v_plane[4 * a:P, :],
-                        start=(a == 0), stop=(a == K_PASSES - 1))
-            else:
-                for b in range(BLOCKS):
-                    nc.tensor.transpose(bank[:, b * P:(b + 1) * P], h_turned[:, b, t, :], ident[:])
             h = ring.tile([P, S], F32, name="h", tag="h", bufs=3)
-            nc.scalar.activation(h[:], bank[:], ACT.Copy, scale=gain_t[:, g, t:t + 1])
-            nc.vector.tensor_tensor(pages[s][:].indirect(idx2[:]), h[:], wg[t], ALU.mult)
+            for cols, entries in (halves if s == 0 else whole_list):
+                bank = psum.tile([P, S], F32, name="h_bank", tag="early", bufs=2)
+                if g == 0:
+                    for a in range(K_PASSES):
+                        nc.tensor.matmul_mx(
+                            out=bank[:, cols], lhsT=w1_dealt[a][:, t, :].bitcast(FP8X4),
+                            lhsT_scale=w1_plane_dealt[4 * a:P, t, :],
+                            rhs=v_codes[a][:, cols].bitcast(FP8X4), rhs_scale=v_plane[4 * a:P, cols],
+                            start=(a == 0), stop=(a == K_PASSES - 1))
+                else:
+                    for b in range(BLOCKS):
+                        nc.tensor.transpose(bank[:, b * P:(b + 1) * P], h_turned[:, b, t, :], ident[:])
+                nc.scalar.activation(h[:, cols], bank[:, cols], ACT.Copy, scale=gain_t[:, g, t:t + 1])
+                nc.vector.tensor_tensor(pages[s][:].indirect(idx2[:, entries]), h[:, cols], wg[t][:, cols], ALU.mult)
 
         x_codes = [keep.tile([P, PICKS], I32, name="x_codes%d" % g, align_bytes=64) for g in range(GROUPS)]
         x_plane = [keep.tile([P, PICKS], U8, name="x_plane%d" % g, align_bytes=64) for g in range(GROUPS)]
@@ -191,21 +206,19 @@ def tile_list_kelp_harvest_planner_kernel(
             if g == 0:
                 picked = keep.tile([P, PACK, PICKS], F32, name="picked")
             else:
-                picked = ring.tile([P, PACK, PICKS], F32, name="picked", tag="big", bufs=4)
+                picked = ring.tile([P, PACK, PICKS], F32, name="picked", tag="large", bufs=4)
             x_rows = ring.tile([P, PACK, PICKS], BF16, name="x_rows", tag="x_rows")
             for t in range(PACK):
                 nc.vector.tensor_copy(picked[:, t, :], pages[g * PACK + t][:].indirect(idx3[:]))
                 bent = ring.tile([P, PICKS], F32, name="bent", tag="bent")
-                nc.scalar.activation(bent[:], picked[:, t, :], ACT.Tanh, scale=rs_t[:, g, t:t + 1])
+                nc.scalar.activation(bent[:], picked[:, t, :], ACT.Tanh, bias=zero_bias[:], scale=rs_t[:, g, t:t + 1])
                 nc.scalar.activation(x_rows[:, t, :], bent[:], ACT.Copy, scale=gx_t[:, g, t:t + 1])
             pieces = BLOCKS if g == GROUPS - 1 else 1
             width = PICKS // pieces
             for n in range(pieces):
                 cols = slice(n * width, (n + 1) * width)
-                nc.scalar.copy(x_woven[g][:, cols, :].rearrange("p (c i) t -> p c t i", i=2),
-                               x_rows[:, :, cols].rearrange("p t (c i) -> p c t i", i=2))
-                nc.vector.quantize_mx(out=x_codes[g][:, cols].bitcast(FP8X4), scales=x_plane[g][:, cols],
-                                      in_=x_woven[g][:, cols, :].rearrange("p c t -> p (c t)"))
+                weave(x_woven[g][:, cols, :], x_rows[:, :, cols])
+                quantise(x_codes[g][:, cols], x_plane[g][:, cols], x_woven[g][:, cols, :])
 
         w3_codes = {}
         w3_plane = {}
@@ -214,13 +227,11 @@ def tile_list_kelp_harvest_planner_kernel(
             woven = ring.tile([P, PASS, PACK], BF16, name="w3_woven", tag="woven", bufs=3, align_bytes=64)
             for half in range(2):
                 cols = slice(half * PASS // 2, (half + 1) * PASS // 2)
-                nc.scalar.copy(woven[:, cols, :].rearrange("p (c i) t -> p c t i", i=2),
-                               w3_raw[q][:, :, cols].rearrange("p t (c i) -> p c t i", i=2))
+                weave(woven[:, cols, :], w3_raw[q][:, :, cols])
             key = divmod(q, 2)
             w3_codes[key] = keep.tile([P, PASS], I32, name="w3_codes%d" % q, align_bytes=64)
             w3_plane[key] = keep.tile([P, PASS], U8, name="w3_plane%d" % q, align_bytes=64)
-            nc.vector.quantize_mx(out=w3_codes[key][:].bitcast(FP8X4), scales=w3_plane[key][:],
-                                  in_=woven[:].rearrange("p c t -> p (c t)"))
+            quantise(w3_codes[key][:], w3_plane[key][:], woven[:])
 
         upstream = {}
 
@@ -239,7 +250,7 @@ def tile_list_kelp_harvest_planner_kernel(
             quantise_w3(q)
         reread(1)
         fetch_upstream(0, 1, "upstream0")
-        fetch_upstream(1, 2, "x_woven1")
+        fetch_upstream(1, EARLY_UPSTREAM - 1, "x_woven1")
 
         y_codes = [keep.tile([P, PICKS], I32, name="y_codes%d" % g, align_bytes=64) for g in range(GROUPS)]
         y_plane = keep.tile([P, GROUPS, PICKS], U8, align_bytes=64)
@@ -258,9 +269,10 @@ def tile_list_kelp_harvest_planner_kernel(
             multiply(season, u, [w3_codes[a, g][:].bitcast(FP8X4) for a in range(GROUPS)],
                      [w3_plane[a, g][:] for a in range(GROUPS)])
             turns[u] = ring.tile([P, 2, P, 2], F32, name="turns", tag="turns", bufs=3)
-            nc.scalar.activation(turns[u][:], pairs_of(season), ACT.Abs, scale=1.0 / (2.0 * math.pi))
-            if u < 5:
-                whole[u] = keep.tile([P, 2, P, 2], U32, name="whole", tag="upstream%d" % (3 + u), align_bytes=64)
+            nc.scalar.activation(turns[u][:], pairs_of(season[:]), ACT.Abs, scale=1.0 / (2.0 * math.pi))
+            if EARLY_UPSTREAM + u < SLICES:
+                whole[u] = keep.tile([P, 2, P, 2], U32, name="whole", tag="upstream%d" % (EARLY_UPSTREAM + u),
+                                     align_bytes=64)
             else:
                 whole[u] = ring.tile([P, 2, P, 2], U32, name="whole", tag="whole", bufs=3)
             nc.scalar.activation(whole[u][:], turns[u][:], ACT.Copy, bias=0.25)
@@ -269,17 +281,18 @@ def tile_list_kelp_harvest_planner_kernel(
             g = u // BLOCKS
             rest = ring.tile([P, 2, P, 2], F32, name="rest", tag="rest")
             nc.vector.tensor_tensor(rest[:], turns[u][:], whole[u][:].bitcast(I32), ALU.subtract)
-            if u < 5:
-                fetch_upstream(3 + u, 1, "upstream%d" % (3 + u))
+            if EARLY_UPSTREAM + u < SLICES:
+                fetch_upstream(EARLY_UPSTREAM + u, 1, "upstream%d" % (EARLY_UPSTREAM + u))
             cosine[u] = ring.tile([P, 2, P, 2], F32, name="cosine", tag="cosine", bufs=3)
             nc.scalar.activation(cosine[u][:], rest[:], ACT.Sin, scale=2.0 * math.pi, bias=0.5 * math.pi)
             growth[u] = psum.tile([P, PASS], F32, name="growth", tag="growth", bufs=3)
-            multiply(growth[u], u, [w2_codes[:, a, 2 * g * PASS:2 * (g + 1) * PASS].bitcast(FP4X4) for a in range(GROUPS)],
+            multiply(growth[u], u,
+                     [w2_codes[:, a, 2 * g * PASS:2 * (g + 1) * PASS].bitcast(FP4X4) for a in range(GROUPS)],
                      [w2_plane[:, a, g * PASS:(g + 1) * PASS] for a in range(GROUPS)])
 
         def turn(u):
             product = ring.tile([P, PACK, P], F32, name="product", tag="product")
-            nc.vector.tensor_tensor(dealt(product[:]), pairs_of(growth[u]), cosine[u][:], ALU.mult)
+            nc.vector.tensor_tensor(dealt(product[:]), pairs_of(growth[u][:]), cosine[u][:], ALU.mult)
             turned[u] = psum.tile([P, PACK, P], F32, name="turned", tag="turned", bufs=3)
             for t in range(PACK):
                 nc.tensor.transpose(turned[u][:, t, :], product[:, t, :], ident[:])
@@ -293,24 +306,21 @@ def tile_list_kelp_harvest_planner_kernel(
                                                turned[u][:, t, :], ALU.mult, ALU.add)
             nc.sync.dma_start(out_rows[g][:, :, cols], y[:])
             y_woven[u] = ring.tile([P, P, PACK], BF16, name="y_woven", tag="woven", bufs=3, align_bytes=64)
-            nc.scalar.copy(y_woven[u][:].rearrange("p (c i) t -> p c t i", i=2),
-                           y[:].rearrange("p t (c i) -> p c t i", i=2))
+            weave(y_woven[u][:], y[:])
 
         def quantise_y(u):
             g, b = divmod(u, BLOCKS)
             cols = slice(b * P, (b + 1) * P)
-            nc.vector.quantize_mx(out=y_codes[g][:, cols].bitcast(FP8X4), scales=y_plane[:, g, cols],
-                                  in_=y_woven[u][:].rearrange("p c t -> p (c t)"))
+            quantise(y_codes[g][:, cols], y_plane[:, g, cols], y_woven[u][:])
             if b % 2 == 1:
                 pair = slice((b - 1) * P, (b + 1) * P)
                 nc.sync.dma_start(out_words[g][:, pair], y_codes[g][:, pair])
 
         stages = [count_turns, take_cosine, turn, finish, quantise_y]
-        units = GROUPS * BLOCKS
-        for step in range(units + len(stages) - 1):
+        for step in range(UNITS + len(stages) - 1):
             for depth, stage in enumerate(stages):
-                if 0 <= step - depth < units:
+                if 0 <= step - depth < UNITS:
                     stage(step - depth)
         for q in range(QUADS):
             nc.scalar.dma_start(out_2[:, 4 * q:4 * q + 4, :].rearrange("g r m -> r g m").bitcast(I32),
-                              y_plane[32 * q:32 * q + 4, :, :].bitcast(I32))
+                                y_plane[32 * q:32 * q + 4, :, :].bitcast(I32))

import math
from contextlib import ExitStack

import concourse.mybir as mybir
from concourse.masks import make_identity

K, T, H, S, T2, PICKS = 1536, 2048, 1024, 512, 1024, 512
FLOPS = 2 * K * H * S + 2 * 2 * H * H * PICKS

F32 = mybir.dt.float32
BF16 = mybir.dt.bfloat16
I32 = mybir.dt.int32
U32 = mybir.dt.uint32
U16 = mybir.dt.uint16
U8 = mybir.dt.uint8
FP8X4 = mybir.dt.float8_e4m3fn_x4
FP4X4 = mybir.dt.float4_e2m1fn_x4
ACT = mybir.ActivationFunctionType
ALU = mybir.AluOpType

P = 128
PACK = 4
PASS = P * PACK
QUADS = 4
K_PASSES = K // PASS
GROUPS = H // PASS
SLICES = GROUPS * PACK
BLOCKS = PICKS // P
UNITS = GROUPS * BLOCKS
LIST_COLS = S // 16
EARLY_UPSTREAM = 3


def tile_list_kelp_harvest_planner_kernel(
    tc, tab_words, tab_scales, w1_words, w1_scales, gain, page0, wgs, rs, gx,
    w2_words, w2_scales, w3, offs, offs2, offs3, offs4, out_0, out_1, out_2,
):
    nc = tc.nc
    with ExitStack() as ctx:
        lists = ctx.enter_context(tc.tile_pool(name="lists", bufs=1))
        keep = ctx.enter_context(tc.tile_pool(name="keep", bufs=1))
        ring = ctx.enter_context(tc.tile_pool(name="ring", bufs=2))
        psum = ctx.enter_context(tc.psum_pool(name="psum", bufs=1))

        w1_cols = w1_words.rearrange("a p c i -> p a (c i)").bitcast(I32)
        page_rows = page0.rearrange("(g p t) c -> g t p c", g=GROUPS, t=PACK)
        wgs_rows = wgs.rearrange("(m t) s -> m t s", t=PACK)
        w3_rows = w3.rearrange("(a p j) n -> a p j n", a=GROUPS, j=PACK)
        out_rows = out_0.rearrange("(g p t) j -> g p t j", g=GROUPS, t=PACK)
        out_words = out_1.rearrange("g p m t -> g p (m t)").bitcast(I32)

        def load_list(source, name):
            tile = lists.tile([P, LIST_COLS], U16, name=name)
            nc.sync.dma_start(tile[:], source)
            return tile

        def load_by_slice(source, name):
            tile = keep.tile([P, GROUPS, PACK], F32, name=name)
            nc.gpsimd.dma_start(tile[:], source.rearrange("(g p t) -> p g t", g=GROUPS, t=PACK))
            return tile

        def load_w1(g):
            tile = ring.tile([P, K_PASSES, PASS], I32, name="w1_raw", tag="w1_raw", align_bytes=64)
            nc.sync.dma_start(tile[:], w1_cols[:, :, g * PASS:(g + 1) * PASS])
            return tile

        def load_tab(a):
            tile = ring.tile([P, T], I32, name="tab", tag="large", bufs=4)
            nc.sync.dma_start(tile[:], tab_words[a].rearrange("p c i -> p (c i)").bitcast(I32))
            return tile

        def load_w3(q):
            tile = ring.tile([P, PACK, PASS], F32, name="w3_raw", tag="large", bufs=4)
            nc.sync.dma_start(tile[:], w3_rows[q // 2][:, :, (q % 2) * PASS:(q % 2 + 1) * PASS])
            return tile

        def load_page(s):
            tile = keep.tile([P, T2], F32, name="page%d" % s)
            nc.sync.dma_start(tile[:], page_rows[s // PACK, s % PACK])
            return tile

        wg = []

        def load_wg(first, count):
            tile = keep.tile([P, count, S], F32, name="wg%d" % first)
            for q in range(QUADS):
                nc.sync.dma_start(tile[32 * q:32 * q + 32, :, :], wgs_rows[:, first:first + count, :])
            wg.extend(tile[:, n, :] for n in range(count))

        tab_plane = keep.tile([P, T], U8, tag="v_codes2", align_bytes=64)
        w1_plane_raw = keep.tile([P, H], U8, tag="v_codes1", align_bytes=64)
        w2_plane = keep.tile([P, GROUPS, H], U8, align_bytes=64)
        silu_input = keep.tile([P, 1], F32)
        nc.gpsimd.memset(w1_plane_raw[:].bitcast(I32), 0)
        nc.gpsimd.memset(tab_plane[:].bitcast(I32), 0)
        nc.vector.memset(silu_input[:], 0.0)
        nc.vector.memset(w2_plane[:].bitcast(I32), 0)
        for q in range(QUADS):
            nc.gpsimd.dma_start(tab_plane[32 * q:32 * q + 4 * K_PASSES, :].bitcast(I32),
                                tab_scales[:, 4 * q:4 * q + 4, :].bitcast(I32))
        for q in range(QUADS):
            nc.scalar.dma_start(w1_plane_raw[32 * q:32 * q + 4 * K_PASSES, :].bitcast(I32),
                                w1_scales[:, 4 * q:4 * q + 4, :].bitcast(I32))
        zero_bias = keep.tile([P, 1], F32)
        nc.scalar.activation(zero_bias[:], silu_input[:], ACT.Silu)
        gain_t = load_by_slice(gain, "gain_t")
        rs_t = load_by_slice(rs, "rs_t")
        gx_t = load_by_slice(gx, "gx_t")
        ident = keep.tile([P, P], F32)
        make_identity(nc, ident[:])

        w1_raw = [load_w1(0)]
        tab = [load_tab(0)]
        idx = load_list(offs, "idx")
        tab.extend(load_tab(a) for a in range(1, K_PASSES))
        idx2 = load_list(offs2, "idx2")
        pages = [load_page(0)]
        load_wg(0, 1)
        pages.append(load_page(1))
        load_wg(1, 1)
        pages.append(load_page(2))
        load_wg(2, 2)
        w1_raw.append(load_w1(1))
        pages.append(load_page(3))
        idx3 = load_list(offs3, "idx3")
        pages.extend(load_page(s) for s in range(PACK, SLICES))
        w3_raw = [load_w3(q) for q in range(2 * GROUPS)]
        w2_codes = keep.tile([P, GROUPS, 2 * H], U8, align_bytes=64)
        nc.sync.dma_start(w2_codes[:].bitcast(I32), w2_words.rearrange("a p b -> p a b").bitcast(I32))
        for q in range(QUADS):
            nc.sync.dma_start(w2_plane[32 * q:32 * q + 4, :, :].bitcast(I32),
                              w2_scales[:, 4 * q:4 * q + 4, :].rearrange("a r n -> r a n").bitcast(I32))
        idx4 = load_list(offs4, "idx4")

        def pairs_of(columns):
            return columns.rearrange("p (m d e) -> p d m e", d=2, e=2)

        def dealt(rows):
            return rows.rearrange("p (d e) m -> p d m e", e=2)

        def weave(woven, rows):
            nc.scalar.copy(woven.rearrange("p (c i) t -> p c t i", i=2), rows.rearrange("p t (c i) -> p c t i", i=2))

        def quantise(codes, plane, woven):
            nc.vector.quantize_mx(out=codes.bitcast(FP8X4), scales=plane, in_=woven.rearrange("p c t -> p (c t)"))

        w1_dealt = []
        for a in range(K_PASSES):
            tile = keep.tile([P, PACK, P], I32, name="w1_dealt%d" % a, align_bytes=64)
            nc.vector.tensor_copy(dealt(tile[:]), pairs_of(w1_raw[0][:, a, :]))
            w1_dealt.append(tile)
        w1_plane_dealt = keep.tile([P, PACK, P], U8, align_bytes=64)
        nc.vector.tensor_copy(w1_plane_dealt[:], w1_plane_raw[:, 0:PASS].rearrange("p (m t) -> p t m", t=PACK))
        w1_plane_rest = keep.tile([P, PASS], U8, align_bytes=64)
        nc.vector.tensor_copy(w1_plane_rest[:].bitcast(I32), w1_plane_raw[:, PASS:H].bitcast(I32))
        v_plane = keep.tile([P, S], U8, align_bytes=64)
        nc.vector.tensor_copy(v_plane[:], tab_plane[:].indirect(idx[:]))

        whole_list = [(slice(0, S), slice(0, LIST_COLS))]
        halves = [(slice(n * S // 2, (n + 1) * S // 2), slice(n * LIST_COLS // 2, (n + 1) * LIST_COLS // 2))
                  for n in range(2)]
        v_codes = []
        for a in range(K_PASSES):
            tile = keep.tile([P, S], I32, name="v_codes%d" % a, tag="v_codes%d" % a, align_bytes=64)
            for cols, entries in (halves if a == K_PASSES - 1 else whole_list):
                nc.vector.tensor_copy(tile[:, cols].bitcast(U32), tab[a][:].bitcast(U32).indirect(idx[:, entries]))
            v_codes.append(tile)

        h_turned = keep.tile([P, BLOCKS, PACK, P], F32)

        def multiply_turned():
            for b in range(BLOCKS):
                cols = slice(b * P, (b + 1) * P)
                bank = psum.tile([P, PASS], F32, name="h_turned_bank", tag="growth", bufs=3)
                for a in range(K_PASSES):
                    nc.tensor.matmul_mx(
                        out=bank[:], lhsT=v_codes[a][:, cols].bitcast(FP8X4), lhsT_scale=v_plane[4 * a:P, cols],
                        rhs=w1_raw[1][:, a, :].bitcast(FP8X4), rhs_scale=w1_plane_rest[4 * a:P, :],
                        start=(a == 0), stop=(a == K_PASSES - 1))
                nc.scalar.copy(dealt(h_turned[:, b, :, :]), pairs_of(bank[:]))

        def put(s):
            g, t = divmod(s, PACK)
            h = ring.tile([P, S], F32, name="h", tag="h", bufs=3)
            for cols, entries in (halves if s == 0 else whole_list):
                bank = psum.tile([P, S], F32, name="h_bank", tag="early", bufs=2)
                if g == 0:
                    for a in range(K_PASSES):
                        nc.tensor.matmul_mx(
                            out=bank[:, cols], lhsT=w1_dealt[a][:, t, :].bitcast(FP8X4),
                            lhsT_scale=w1_plane_dealt[4 * a:P, t, :],
                            rhs=v_codes[a][:, cols].bitcast(FP8X4), rhs_scale=v_plane[4 * a:P, cols],
                            start=(a == 0), stop=(a == K_PASSES - 1))
                else:
                    for b in range(BLOCKS):
                        nc.tensor.transpose(bank[:, b * P:(b + 1) * P], h_turned[:, b, t, :], ident[:])
                nc.scalar.activation(h[:, cols], bank[:, cols], ACT.Copy, scale=gain_t[:, g, t:t + 1])
                nc.vector.tensor_tensor(pages[s][:].indirect(idx2[:, entries]), h[:, cols], wg[t][:, cols], ALU.mult)

        x_codes = [keep.tile([P, PICKS], I32, name="x_codes%d" % g, align_bytes=64) for g in range(GROUPS)]
        x_plane = [keep.tile([P, PICKS], U8, name="x_plane%d" % g, align_bytes=64) for g in range(GROUPS)]
        x_woven = [keep.tile([P, PICKS, PACK], BF16, name="x_woven%d" % g, tag="x_woven%d" % g, align_bytes=64)
                   for g in range(GROUPS)]

        def reread(g):
            if g == 0:
                picked = keep.tile([P, PACK, PICKS], F32, name="picked")
            else:
                picked = ring.tile([P, PACK, PICKS], F32, name="picked", tag="large", bufs=4)
            x_rows = ring.tile([P, PACK, PICKS], BF16, name="x_rows", tag="x_rows")
            for t in range(PACK):
                nc.vector.tensor_copy(picked[:, t, :], pages[g * PACK + t][:].indirect(idx3[:]))
                bent = ring.tile([P, PICKS], F32, name="bent", tag="bent")
                nc.scalar.activation(bent[:], picked[:, t, :], ACT.Tanh, bias=zero_bias[:], scale=rs_t[:, g, t:t + 1])
                nc.scalar.activation(x_rows[:, t, :], bent[:], ACT.Copy, scale=gx_t[:, g, t:t + 1])
            pieces = BLOCKS if g == GROUPS - 1 else 1
            width = PICKS // pieces
            for n in range(pieces):
                cols = slice(n * width, (n + 1) * width)
                weave(x_woven[g][:, cols, :], x_rows[:, :, cols])
                quantise(x_codes[g][:, cols], x_plane[g][:, cols], x_woven[g][:, cols, :])

        w3_codes = {}
        w3_plane = {}

        def quantise_w3(q):
            woven = ring.tile([P, PASS, PACK], BF16, name="w3_woven", tag="woven", bufs=3, align_bytes=64)
            for half in range(2):
                cols = slice(half * PASS // 2, (half + 1) * PASS // 2)
                weave(woven[:, cols, :], w3_raw[q][:, :, cols])
            key = divmod(q, 2)
            w3_codes[key] = keep.tile([P, PASS], I32, name="w3_codes%d" % q, align_bytes=64)
            w3_plane[key] = keep.tile([P, PASS], U8, name="w3_plane%d" % q, align_bytes=64)
            quantise(w3_codes[key][:], w3_plane[key][:], woven[:])

        upstream = {}

        def fetch_upstream(first, count, tag):
            tile = keep.tile([P, count, PICKS], F32, name="upstream%d" % first, tag=tag, align_bytes=64)
            for n in range(count):
                upstream[first + n] = tile[:, n, :]
                nc.vector.tensor_copy(tile[:, n, :], pages[first + n][:].indirect(idx4[:]))

        for s in range(SLICES):
            if s == PACK - 1:
                multiply_turned()
            put(s)
        reread(0)
        for q in range(2 * GROUPS):
            quantise_w3(q)
        reread(1)
        fetch_upstream(0, 1, "upstream0")
        fetch_upstream(1, EARLY_UPSTREAM - 1, "x_woven1")

        y_codes = [keep.tile([P, PICKS], I32, name="y_codes%d" % g, align_bytes=64) for g in range(GROUPS)]
        y_plane = keep.tile([P, GROUPS, PICKS], U8, align_bytes=64)
        turns, whole, cosine, growth, turned, y_woven = {}, {}, {}, {}, {}, {}

        def multiply(bank, u, codes, plane):
            cols = slice(u % BLOCKS * P, (u % BLOCKS + 1) * P)
            for a in range(GROUPS):
                nc.tensor.matmul_mx(
                    out=bank[:], lhsT=x_codes[a][:, cols].bitcast(FP8X4), lhsT_scale=x_plane[a][:, cols],
                    rhs=codes[a], rhs_scale=plane[a], start=(a == 0), stop=(a == GROUPS - 1))

        def count_turns(u):
            g = u // BLOCKS
            season = psum.tile([P, PASS], F32, name="season", tag="early", bufs=2)
            multiply(season, u, [w3_codes[a, g][:].bitcast(FP8X4) for a in range(GROUPS)],
                     [w3_plane[a, g][:] for a in range(GROUPS)])
            turns[u] = ring.tile([P, 2, P, 2], F32, name="turns", tag="turns", bufs=3)
            nc.scalar.activation(turns[u][:], pairs_of(season[:]), ACT.Abs, scale=1.0 / (2.0 * math.pi))
            if EARLY_UPSTREAM + u < SLICES:
                whole[u] = keep.tile([P, 2, P, 2], U32, name="whole", tag="upstream%d" % (EARLY_UPSTREAM + u),
                                     align_bytes=64)
            else:
                whole[u] = ring.tile([P, 2, P, 2], U32, name="whole", tag="whole", bufs=3)
            nc.scalar.activation(whole[u][:], turns[u][:], ACT.Copy, bias=0.25)

        def take_cosine(u):
            g = u // BLOCKS
            rest = ring.tile([P, 2, P, 2], F32, name="rest", tag="rest")
            nc.vector.tensor_tensor(rest[:], turns[u][:], whole[u][:].bitcast(I32), ALU.subtract)
            if EARLY_UPSTREAM + u < SLICES:
                fetch_upstream(EARLY_UPSTREAM + u, 1, "upstream%d" % (EARLY_UPSTREAM + u))
            cosine[u] = ring.tile([P, 2, P, 2], F32, name="cosine", tag="cosine", bufs=3)
            nc.scalar.activation(cosine[u][:], rest[:], ACT.Sin, scale=2.0 * math.pi, bias=0.5 * math.pi)
            growth[u] = psum.tile([P, PASS], F32, name="growth", tag="growth", bufs=3)
            multiply(growth[u], u,
                     [w2_codes[:, a, 2 * g * PASS:2 * (g + 1) * PASS].bitcast(FP4X4) for a in range(GROUPS)],
                     [w2_plane[:, a, g * PASS:(g + 1) * PASS] for a in range(GROUPS)])

        def turn(u):
            product = ring.tile([P, PACK, P], F32, name="product", tag="product")
            nc.vector.tensor_tensor(dealt(product[:]), pairs_of(growth[u][:]), cosine[u][:], ALU.mult)
            turned[u] = psum.tile([P, PACK, P], F32, name="turned", tag="turned", bufs=3)
            for t in range(PACK):
                nc.tensor.transpose(turned[u][:, t, :], product[:, t, :], ident[:])

        def finish(u):
            g, b = divmod(u, BLOCKS)
            cols = slice(b * P, (b + 1) * P)
            y = ring.tile([P, PACK, P], F32, name="y", tag="y", bufs=3)
            for t in range(PACK):
                nc.vector.scalar_tensor_tensor(y[:, t, :], upstream[g * PACK + t][:, cols], rs_t[:, g, t:t + 1],
                                               turned[u][:, t, :], ALU.mult, ALU.add)
            nc.sync.dma_start(out_rows[g][:, :, cols], y[:])
            y_woven[u] = ring.tile([P, P, PACK], BF16, name="y_woven", tag="woven", bufs=3, align_bytes=64)
            weave(y_woven[u][:], y[:])

        def quantise_y(u):
            g, b = divmod(u, BLOCKS)
            cols = slice(b * P, (b + 1) * P)
            quantise(y_codes[g][:, cols], y_plane[:, g, cols], y_woven[u][:])
            if b % 2 == 1:
                pair = slice((b - 1) * P, (b + 1) * P)
                nc.sync.dma_start(out_words[g][:, pair], y_codes[g][:, pair])

        stages = [count_turns, take_cosine, turn, finish, quantise_y]
        for step in range(UNITS + len(stages) - 1):
            for depth, stage in enumerate(stages):
                if 0 <= step - depth < UNITS:
                    stage(step - depth)
        for q in range(QUADS):
            nc.scalar.dma_start(out_2[:, 4 * q:4 * q + 4, :].rearrange("g r m -> r g m").bitcast(I32),
                                y_plane[32 * q:32 * q + 4, :, :].bitcast(I32))
